import numpy as np, ml_dtypes
CORES = [66,74,82,90,194,202,210,218]
N = 8
BF = ml_dtypes.bfloat16
def gentries(a):
    return np.ascontiguousarray(a.reshape(8, 16, -1).transpose(0, 2, 1)).reshape(8, -1)
def gtable(e):
    e = np.asarray(e); return np.ascontiguousarray(e.reshape(8, -1, 16).transpose(0, 2, 1)).reshape(128, -1).astype(np.int32)
W, M, H, SC, TH, CAP, RO = 2048, 320, 12, 16, 76, 80, 4
B = 8
LEV = np.arange(H).reshape(1, 1, H, 1)
def parts(rng):
    weak = rng.random((N, 8, 1, W)) < rng.choice(np.array([0.15, 0.3, 0.5]), (N, 8, 1, 1))
    size = np.where(weak, 0.25, rng.choice(np.array([0.5, 1.0]), (N, 8, 1, W)))
    s = (256 * size * rng.random((N, 8, 16, W))).astype(np.int64); w = rng.integers(0, 256, (N, 8, 16, W))
    c = rng.integers(0, W, (N, 8, H, M)); n = rng.integers(1, H + 1, (N, 8, M)); to = np.argsort(rng.random((N, 8, M)), axis=-1)
    return s, w, c, n, to
def pack(s, w, c, n, to):
    return {"st": s.reshape(N, 128, W).astype(np.float32).astype(BF), "wt": w.reshape(N, 128, W).astype(np.float32).astype(BF),
            "cs": np.stack([gtable(a.reshape(8, -1)) for a in c]), "ns": np.stack([gtable(a) for a in n]), "ds": np.stack([gtable(a) for a in to])}
def plant(rng, s, w, edge):
    k = 17 * B; pc = 1 + np.argsort(rng.random((N, 8, W - 1)), axis=-1)[..., :k]
    yes = (np.argsort(rng.random((N, 8, k, 16)), axis=-1) < np.repeat(np.arange(17), B)[:, None]).transpose(0, 1, 3, 2)
    ix = np.ascontiguousarray(np.broadcast_to(pc[:, :, None, :], (N, 8, 16, k)))
    if edge:
        a = rng.integers(1, 256 // SC, yes.shape); b = SC * a + yes
    else:
        a = np.where(yes, 0, 255); b = rng.integers(1, 256, yes.shape)
    np.put_along_axis(s, ix, a, 3); np.put_along_axis(w, ix, b, 3); s[..., 0] = 255
    return pc
def stacks(rng, pc, j):
    e = np.take_along_axis(pc, (j * B + rng.integers(0, B, j.shape)).reshape(N, 8, H * M), 2).reshape(j.shape)
    return np.where(LEV % 2 == 1, e, 0)
def setup_inputs(rng):
    return pack(*parts(rng))
def setup_inputs_room(rng):
    s, w, c, n, to = parts(rng); pc = plant(rng, s, w, False); n = rng.integers(2, H + 1, (N, 8, M))
    cnt = rng.permuted(np.tile(np.array([M, M // 2, M // 2, CAP + 1, CAP, CAP - 1, 1, 0]), (N, 1)), axis=1)
    pos = np.argsort(rng.random((N, 1, M)), axis=-1)
    top = np.where(pos < cnt[:, :, None], 16, 8)[:, :, None]
    kk = (1 + 2 * (rng.integers(0, H, (N, 8, M)) % (n // 2)))[:, :, None]
    j = np.where(LEV == kk, top, np.minimum(rng.integers(0, 17, (N, 8, H, M)), top))
    return pack(s, w, stacks(rng, pc, j), n, to)
def setup_inputs_ties(rng):
    s, w, c, n, to = parts(rng); pc = plant(rng, s, w, True)
    goal = TH - 1 + rng.integers(0, 3, (N, 1, M)); j = goal // 8 + (np.arange(8)[:, None] < goal % 8)
    e = rng.integers(0, min(15 - (TH + 1) // 8, (TH - 1) // 8) + 1, (N, 4, M))
    j = rng.permuted(np.concatenate([j[:, :4] + e, j[:, 4:] - e], axis=1), axis=1)
    m = np.arange(M); h = M // 2
    n = np.where(m < CAP // 4, rng.integers(4, H + 1, (N, 8, M)), np.where(m < h, 2, n))
    c = np.where(m < h, stacks(rng, pc, np.repeat(j[:, :, None], H, axis=2)), c)
    return pack(s, w, c, n, to)
def setup_inputs_alike(rng):
    s, w, c, n, to = parts(rng); half = rng.random((N, 1, M)) < 0.5
    n = np.where(half, rng.choice(np.array([1, 2, H - 1, H]), (N, 8, M)), n)
    c = np.where(half[:, :, None], rng.choice(np.array([0, 1, W // 2, W - 1]), (N, 8, H, M)), c)
    i = np.arange(M); to[:, 0] = i; to[:, 1] = i[::-1]; to[:, 2] = (i + 1) % M
    w[:, 3] = 255 * rng.integers(0, 2, (N, 16, W))
    return pack(s, w, c, n, to)
def setup_inputs_full(rng):
    s, w, c, n, to = parts(rng)
    n = np.where(rng.random((N, 8, M)) < 0.9, H - rng.integers(0, 2, (N, 8, M)), n)
    q = int(rng.integers(0, N)); a = (q + 1) % N; b = (q + int(rng.integers(2, N))) % N; g = rng.permutation(8)
    n[b, g[0]] = 1; s[q, g[1]] = 255
    n[a, g[1]] = H; c[a, g[1]] -= c[a, g[1]] % 2
    w[a, g[1], :, ::2] = 0; s[a, g[1], :, 1::2] = 0
    x = np.append(rng.permutation(M - 1)[:CAP - 1], M - 1); y = 1 + 2 * rng.integers(0, W // 2, (8, CAP))
    for k in range(8):
        c[a, k, 0, x] = 0; c[a, k, 1, x] = y[k]; n[a, k, x] = np.maximum(n[a, k, x], 2)
        sk = s[a, k]; wk = w[a, k]
        sk[:, y[k]] = 0; wk[:, y[k]] = np.maximum(wk[:, y[k]], 1)
    return pack(s, w, c, n, to)
def setup_inputs_spread(rng):
    s, w, c, n, to = parts(rng)
    s = (np.exp2(8 * rng.random((N, 8, 1, W))) * rng.random((N, 8, 16, W))).astype(np.int64)
    w = (np.exp2(8 * rng.random((N, 8, 1, W))) * rng.random((N, 8, 16, W))).astype(np.int64)
    return pack(s, w, c, n, to)
def check_inputs(d):
    bad = []
    for k in ("st", "wt"):
        a = np.asarray(d[k]).astype(np.float32)
        if not (np.all(a >= 0) and np.all(a <= 255) and np.all(a == np.floor(a))): bad.append("whole numbers of " + k)
    for k, lo, hi in (("cs", 0, W - 1), ("ns", 1, H), ("ds", 0, M - 1)):
        if np.min(d[k]) < lo or np.max(d[k]) > hi: bad.append("range of " + k)
    if np.any(np.sort(np.stack([gentries(a) for a in d["ds"]]), axis=-1) != np.arange(M)): bad.append("targets of a group differ")
    return bad
def reference(st, wt, cs, ns, ds):
    s = st.astype(np.float32).astype(np.int32).reshape(N, 8, 16, W); w = wt.astype(np.float32).astype(np.int32).reshape(N, 8, 16, W)
    c = np.stack([gentries(a) for a in cs]).astype(np.int64).reshape(N, 8, H, M); n = np.stack([gentries(a) for a in ns]).astype(np.int64)
    inv = np.argsort(np.stack([gentries(a) for a in ds]), axis=-1)
    imp = np.zeros((N, 8, 16, M), np.int64); site = np.arange(M)
    for t in range(RO):
        live = LEV < n[:, :, None]; c = np.where(live, c, 0)
        rho = np.take_along_axis(w, c.reshape(N, 8, 1, H * M), 3).reshape(N, 8, 16, H, M) * live[:, :, None]
        own = np.add.accumulate(rho[:, :, :, ::-1], axis=3)[:, :, :, ::-1]
        low = np.concatenate([c[:, :, :1], c[:, :, :-1]], axis=2)
        h = (((c * low) >> 5) + c + 77 * t) & (W - 1)
        over = own + imp[:, :, :, None] > SC * np.take_along_axis(s, h.reshape(N, 8, 1, H * M), 3).reshape(N, 8, 16, H, M)
        v = np.where(live & (LEV > 0), np.add.reduce(over.astype(np.int64), axis=2), 0)
        most = np.max(v, axis=2); ks = np.argmax(v, axis=2)
        c = np.where(live, (13 * c + 97 * v + t) & (W - 1), 0)
        ready = (most >= 9) & (np.add.reduce(most, axis=1, keepdims=True) >= TH); one = ready.astype(np.int64)
        slide = ready & (np.add.accumulate(one, axis=2) - one < CAP)
        load = np.take_along_axis(own, ks[:, :, None, None], 3)[:, :, :, 0]
        old = n; grow = ~slide & (old < H)
        top = np.take_along_axis(c, old[:, :, None] - 1, 2)[:, :, 0]
        e = np.where(grow[:, :, None] & (LEV == old[:, :, None]), ((31 * site + 997 * t + top) & (W - 1))[:, :, None], c)
        n = np.where(slide, ks, old + grow)
        nc, nn, ni = [], [], []
        for a in range(N):
            q = (a - 1 - t % (N - 1)) % N; i = inv[q]
            got = np.take_along_axis(slide[q], i, 1); k0 = np.take_along_axis(ks[q], i, 1); end = np.take_along_axis(old[q], i, 1)
            row = LEV[0] - n[a][:, None] + k0[:, None]
            run = np.take_along_axis(np.take_along_axis(c[q], i[:, None], 2), np.clip(row, 0, H - 1), 1)
            hit = got[:, None] & (row >= k0[:, None]) & (row < end[:, None])
            nc.append(np.where(hit, run, e[a])); nn.append(np.minimum(n[a] + got * (end - k0), H))
            ni.append(np.take_along_axis(load[q], i[:, None], 2) * got[:, None])
        c = np.stack(nc); n = np.stack(nn); imp = np.stack(ni)
    c = np.where(LEV < n[:, :, None], c, -1)
    return {"yc": np.stack([gtable(a.reshape(8, -1)) for a in c]).astype(np.float32), "yn": np.stack([gtable(a) for a in n]).astype(np.float32), "yi": imp.reshape(N, 128, M).astype(np.float32)}

@@ -1,0 +1,496 @@
+from concourse.mybir import AluOpType, ActivationFunctionType
+
+A = AluOpType
+F = ActivationFunctionType
+RO = 4
+UPPER = (7, 5, 3)
+U = 4096.0
+OFF = 1408.0
+BIG = 65536.0
+
+SCRATCH = {}
+for _dt, _bufs in (
+        ("int32", dict(CS=240, NS=32, DS=32, P=224, Q=224, TT=240, CN=240, SI=64, G3=240, G4=240, X=128, X2=128, PC=8,
+                       JI=64, HJ=16)),
+        ("bfloat16", dict(WT=2064, ST=2048, S16=2320, WU=3520, WL=960, SG=3520, L2=320, OVER=3840, KB=32, RD=32, CUM=32,
+                          Z=144, ID=128, NI=128, GS=128, BO=128, TR=128, NB=128, KK=240, NEG=32, ONE=128)),
+        ("float16", dict(IMP=320, XT=320, NH=128)),
+        ("uint16", dict(WI=224, HI=224, AL=32, IL=32, PL=32, LBC=16, LMG=16, LBA=48, LBU=32, LY=32)),
+        ("float32", dict(C=256, NU=32, L1=320, OWN=3520, C13=240, KS=240, WB=240, M60=64, M61=64, SM=640, B=352, KW=672,
+                         Y=320, O0=224, O1=224, CA=224, G1=224, G2=224, V4=240, R1=224, QQ=224, V0=224, YI=320, PF=16,
+                         IF=128, KU=256, GSC=224, J=64, J1=64, J2=64, J3=64, J4=32, H=64))):
+    for _n, _w in _bufs.items():
+        SCRATCH[_n] = ("sbuf", [128, _w], _dt)
+PSUM = ("K0", "K1", "K2", "K3", "ACC", "TOT", "POS", "EX")
+for _n in PSUM:
+    SCRATCH[_n] = ("psum", [128, 512], "float32")
+for _t in range(RO):
+    SCRATCH["MK%d" % _t] = ("sbuf", [128, 320], "float16")
+    SCRATCH["RK%d" % _t] = ("sbuf", [128, 320], "float16")
+    SCRATCH["ML%d" % _t] = ("sbuf", [128, 328], "float32")
+    SCRATCH["RL%d" % _t] = ("sbuf", [128, 328], "float32")
+SEMAPHORES = (["v", "a", "t", "p", "sent", "d_cs", "d_ns", "d_ds", "d_wt", "d_s0", "d_s1", "d_yc", "d_yn", "d_yi"]
+              + ["rk%d" % t for t in range(RO)] + ["rl%d" % t for t in range(RO)])
+
+
+def rank_program(g, core, T, topo):
+    rank = T.rank_of(core)
+    if rank is None:
+        return
+    n_ranks = len(T.cores)
+    eng = {"v": g.vector, "a": g.scalar, "t": g.tensor, "p": g, "s": g.sync}
+    count = {"v": 0, "a": 0, "t": 0, "p": 0}
+    known = {q: {} for q in eng}
+    snap = {}
+    log = {}
+
+    def r(name, lo, hi, step=1):
+        ap = T[name][:, lo:hi] if step == 1 else T[name][:, lo:hi:step]
+        if name in PSUM:
+            return ap, [(name, 0, 512)]
+        return ap, [(name, lo, hi)]
+
+    def ind(win, off):
+        return win[0].indirect(off[0]), win[1] + off[1]
+
+    def sm(i):
+        return r("SM", 32 * i, 32 * i + 20)
+
+    def wait(q, sem, val):
+        if known[q].get(sem, 0) >= val:
+            return
+        eng[q].wait_ge(T.sem[sem], val)
+        known[q][sem] = val
+        for s2, v2 in snap.get((sem, val), {}).items():
+            if known[q].get(s2, 0) < v2:
+                known[q][s2] = v2
+
+    def order(q, reads, writes):
+        need = {}
+        for rs, w in ((reads, False), (writes, True)):
+            for name, lo, hi in rs:
+                ps = name in PSUM
+                for lo2, hi2, w2, sem, val in log.get(name, []):
+                    if lo < hi2 and lo2 < hi and (w or w2 or (ps and sem != q)):
+                        if q == "t" and sem == "t":
+                            continue
+                        need[sem] = max(need.get(sem, 0), val)
+        for sem in sorted(need, key=lambda s: s == q):
+            wait(q, sem, need[sem])
+
+    def note(q, reads, writes, sem, val, keep=False):
+        snap[(sem, val)] = dict(known[q])
+        for name, lo, hi in writes:
+            log[name] = [e for e in log.get(name, []) if keep or not (lo <= e[0] and e[1] <= hi)] + [(lo, hi, True, sem, val)]
+        for name, lo, hi in reads:
+            log[name] = [e for e in log.get(name, []) if not (e[3] == sem and not e[2] and lo <= e[0] and e[1] <= hi)]
+            log[name].append((lo, hi, False, sem, val))
+
+    def emit(q, make, reads, writes, inc=True, apart=None):
+        if apart is None:
+            order(q, reads, writes)
+        else:
+            order(q, reads, [])
+            wait(q, apart[0], apart[1])
+        ins = make()
+        if inc:
+            count[q] += 1
+            ins.then_inc(T.sem[q], 1)
+            note(q, reads, writes, q, count[q], apart is not None)
+        else:
+            note(q, reads, writes, q, count[q] + 1)
+
+    def tt(out, a, b, op, apart=None):
+        emit("v", lambda: g.vector.tensor_tensor(out[0], a[0], b[0], op), a[1] + b[1], out[1], True, apart)
+
+    def ts(out, a, s1, op0, s2=None, op1=None, apart=None):
+        rd = a[1] + (s1[1] if isinstance(s1, tuple) else []) + (s2[1] if isinstance(s2, tuple) else [])
+        x1 = s1[0] if isinstance(s1, tuple) else s1
+        x2 = s2[0] if isinstance(s2, tuple) else s2
+        if op1 is None:
+            emit("v", lambda: g.vector.tensor_scalar(out[0], a[0], x1, None, op0), rd, out[1], True, apart)
+        else:
+            emit("v", lambda: g.vector.tensor_scalar(out[0], a[0], x1, x2, op0, op1), rd, out[1], True, apart)
+
+    def cp(out, a, apart=None):
+        emit("v", lambda: g.vector.tensor_copy(out[0], a[0]), a[1], out[1], True, apart)
+
+    def tr(out, a):
+        emit("v", lambda: g.vector.transpose(out[0], a[0]), a[1], out[1])
+
+    def fill(out, val):
+        emit("v", lambda: g.vector.memset(out[0], val), [], out[1])
+
+    def act(out, a, func=F.Identity, bias=0.0, scale=1.0, apart=None):
+        emit("a", lambda: g.scalar.activation(out[0], a[0], func, bias=float(bias), scale=float(scale)), a[1], out[1], True, apart)
+
+    def mm(out, lhs, rhs, start, stop, inc=True):
+        emit("t", lambda: g.tensor.matmul(out[0], lhs[0], rhs[0], start, stop), lhs[1] + rhs[1], out[1], inc)
+
+    def iota(out, pattern, base, mult=0, flt=True):
+        if flt:
+            emit("p", lambda: g.iota(out[0], pattern, base, mult, allow_small_or_imprecise_dtypes=True), [], out[1])
+        else:
+            emit("p", lambda: g.iota(out[0], pattern, base, mult), [], out[1])
+
+    def pick(out, a, pattern, op, base, mult, other=0.0):
+        emit("p", lambda: g.affine_select(out[0], a[0], pattern, op, other, base, mult), a[1], out[1])
+
+    def load(q, sem, dst, src):
+        eng[q].dma_start(dst[0], src).then_inc(T.sem[sem], 16)
+        note(q, [], dst[1], sem, 16)
+
+    def store(q, sem, dst, src):
+        order(q, src[1], [])
+        eng[q].dma_start(dst, src[0]).then_inc(T.sem[sem], 16)
+
+    sent = [0]
+
+    def send(t, src, dst, sem):
+        to = T.cores[(rank + 1 + t % (n_ranks - 1)) % n_ranks]
+        rid, pid = topo.addr(to, core)
+        order("p", [(src, 0, 328)], [])
+        g.remote_dma(T[dst][:], T[src][:], T.sem[sem], T.sem.sent, pid, rid, topo.mask(core, to))
+        sent[0] += len(topo.engines(core, to))
+
+    def arrival(t, name, sem):
+        frm = T.cores[(rank - 1 - t % (n_ranks - 1)) % n_ranks]
+        log[name] = [(0, 328, True, sem, len(topo.engines(frm, core)))]
+
+    (KEY1, KEY, THR, FR, SL, A1, A2, LEN, N1, DK, N4, D0, D1, BETA, LS, SC, S8, TMP, KST) = range(19)
+
+    load("s", "d_cs", r("CS", 0, 240), T.cs[:])
+    load("s", "d_ns", r("NS", 0, 20), T.ns[:])
+    load("s", "d_ds", r("DS", 0, 20), T.ds[:])
+    load("s", "d_wt", r("WT", 16, 2064), T.wt[:])
+    load("s", "d_s0", r("ST", 0, 1024), T.st[:, 0:1024])
+    load("s", "d_s1", r("ST", 1024, 2048), T.st[:, 1024:2048])
+
+    iota(r("PC", 0, 1), [[0, 1]], 0, 1, False)
+    iota(r("H", 0, 16), [[16, 16]], 0)
+    iota(r("J", 0, 48), [[0, 6], [16, 8]], 0)
+    iota(r("KU", 0, 240), [[4096, 12], [0, 20]], 1)
+    iota(r("J4", 0, 20), [[1, 20]], 0)
+    iota(r("X", 0, 128), [[1, 128]], 0, 0, False)
+    fill(r("ONE", 0, 128), 1.0)
+    fill(r("WT", 0, 16), 0.0)
+    fill(r("IMP", 0, 320), -OFF)
+    pick(r("ID", 0, 128), r("ONE", 0, 128), [[-1, 128]], A.is_equal, 0, 1)
+    iota(r("YI", 0, 320), [[32, 10], [1024, 2], [1, 16]], 0)
+    for k in range(1, 12):
+        if k not in UPPER:
+            act(r("WU", (k - 1) * 320, k * 320), r("IMP", 0, 320), F.Identity, 0.0, 0.0)
+    act(r("OVER", 0, 320), r("IMP", 0, 320), F.Identity, 0.0, 0.0)
+    act(r("Z", 0, 144), r("IMP", 0, 144), F.Identity, 0.0, 0.0)
+    act(r("NEG", 0, 32), r("IMP", 0, 32), F.Identity, -7328.0, 0.0)
+    act(r("CUM", 0, 32), r("IMP", 0, 32), F.Identity, 0.0, 0.0)
+    act(r("NI", 0, 128), r("ID", 0, 128), F.Identity, 0.0, -1.0)
+    pick(r("BO", 0, 128), r("ONE", 0, 128), [[-16, 8], [0, 16]], A.is_ge, 0, 1)
+    pick(r("BO", 0, 128), r("BO", 0, 128), [[16, 8], [0, 16]], A.is_ge, 15, -1)
+    iota(r("KK", 0, 240), [[-1, 12], [0, 20]], 11)
+    iota(r("GSC", 0, 220), [[0, 11], [496, 20]], 0)
+    iota(r("KU", 240, 244), [[0, 4]], 0)
+    iota(r("WB", 0, 60), [[0, 60]], 0)
+    iota(r("B", 0, 16), [[0, 16]], 0)
+    iota(r("B", 336, 352), [[0, 16]], 0)
+    for t in range(RO):
+        iota(r("ML%d" % t, 0, 8), [[0, 8]], 0)
+
+    ts(r("PC", 1, 2), r("PC", 0, 1), 15, A.bitwise_and)
+    ts(r("PC", 2, 3), r("PC", 0, 1), 16, A.bitwise_and)
+    fill(r("S16", 2304, 2320), 1.0e6)
+    cp(r("PF", 0, 3), r("PC", 0, 3))
+    rc = r("PF", 1, 2)
+    for i, q in enumerate((0, -15, -7, -3, -1, 0)):
+        fill(r("J1", 8 * i, 8 * i + 8), float((q - 2) % 11))
+        if i == 0:
+            ts(r("H", 0, 16), r("H", 0, 16), rc, A.add)
+        if i == 1:
+            ts(r("J", 0, 48), r("J", 0, 48), rc, A.add)
+        if i == 2:
+            ts(r("HJ", 0, 16), r("H", 0, 16), -9.5, A.add, 0.05, A.mult)
+        if i == 3:
+            ts(r("JI", 0, 48), r("J", 0, 48), -4.5, A.add, 0.1, A.mult)
+        if i == 4:
+            ts(r("H", 16, 32), r("HJ", 0, 16), -20.0, A.mult)
+    ts(r("J2", 0, 48), r("JI", 0, 48), -10.0, A.mult)
+    tt(r("H", 32, 48), r("H", 16, 32), r("H", 0, 16), A.add)
+    tt(r("J1", 0, 48), r("J1", 0, 48), r("JI", 0, 48), A.subtract)
+    cp(r("LBC", 0, 16), r("H", 32, 48))
+    tt(r("J2", 0, 48), r("J2", 0, 48), r("J", 0, 48), A.add)
+    ts(r("J3", 0, 48), r("J1", 0, 48), 0.0, A.is_lt, 11.0, A.mult)
+    ts(r("H", 48, 64), r("H", 32, 48), 9.5, A.is_gt, 102.0, A.mult)
+    tt(r("J1", 0, 48), r("J1", 0, 48), r("J3", 0, 48), A.add)
+    ts(r("H", 16, 32), r("HJ", 0, 16), 10.0, A.mult)
+    cp(r("J1", 0, 8), r("JI", 0, 8))
+    tt(r("H", 48, 64), r("H", 48, 64), r("H", 32, 48), A.add)
+    ts(r("J2", 0, 16), r("J2", 0, 16), 16.0, A.mult, 1.0, A.add)
+    ts(r("J1", 16, 48), r("J1", 16, 48), 10.0, A.mult)
+    tt(r("H", 48, 64), r("H", 48, 64), r("H", 16, 32), A.add)
+    ts(r("PF", 4, 5), rc, 31.0, A.mult)
+    tt(r("J1", 0, 48), r("J1", 0, 48), r("J2", 0, 48), A.add)
+    ts(r("LMG", 0, 16), r("H", 48, 64), 223.0, A.min)
+    ts(r("PF", 5, 6), rc, 11.0, A.min, 20.0, A.mult)
+    ts(r("LBA", 0, 16), r("J1", 0, 16), 159.0, A.min)
+    ts(r("LBA", 16, 48), r("J1", 16, 48), 111.0, A.min)
+    ts(r("PF", 6, 7), r("PF", 2, 3), 64.0, A.mult)
+    ts(r("PF", 7, 8), r("PF", 2, 3), -2.0, A.mult, 352.0, A.add)
+    ts(r("LBU", 0, 20), r("J4", 0, 20), r("PF", 5, 6), A.add)
+    cp(r("LY", 0, 20), r("J4", 0, 20))
+    ts(sm(SC), r("J4", 0, 20), 16.0, A.mult, rc, A.add)
+    ts(r("NU", 0, 20), r("NS", 0, 20), U, A.mult)
+    ts(sm(S8), sm(SC), 8.0, A.add)
+    tt(r("V4", 0, 240), ind(r("NU", 0, 20), r("LBC", 0, 15)), r("KU", 0, 240), A.subtract)
+    ts(r("X2", 0, 128), r("X", 0, 128), 15, A.bitwise_and)
+    tt(r("V4", 0, 240), r("V4", 0, 240), r("CS", 0, 240), A.min)
+    ts(r("GS", 0, 128), r("X2", 0, 128), rc, A.is_equal)
+    ts(r("C", 0, 240), r("V4", 0, 240), -1.0, A.max)
+
+    def invert_targets(chain):
+        cp(r("AL", 0, 20), r("DS", 0, 20))
+        chain(11)
+        sc = ind(r("Y", 0, 320), r("AL", 0, 20))
+        emit("v", lambda: g.vector.tensor_copy(sc[0], T.YI[:, 0:320]), [("YI", 0, 320), ("AL", 0, 20)], [("Y", 0, 320)])
+        chain(10)
+        tr(r("KW", 0, 320), r("Y", 0, 320))
+        ts(r("GSC", 0, 220), r("GSC", 0, 220), r("PF", 4, 5), A.add)
+        cp(r("SI", 0, 20), r("KW", 0, 320, 16))
+        chain(9)
+        ts(r("SI", 20, 40), r("SI", 0, 20), 1024, A.bitwise_and)
+        ts(r("SI", 40, 60), r("SI", 0, 20), 1023, A.bitwise_and)
+        ts(sm(A1), r("SI", 20, 40), r("PF", 6, 7), A.not_equal, r("PF", 7, 8), A.mult)
+        ts(r("SI", 41, 60, 2), r("SI", 41, 60, 2), 16.0, A.add)
+        chain(8)
+        tt(sm(A2), sm(A1), r("SI", 40, 60), A.add)
+        cp(r("PL", 0, 20), sm(A2))
+
+    def row(name, k):
+        return r(name, (k - 1) * 320, k * 320)
+
+    def lower(k):
+        i = UPPER.index(k + 1)
+        return r("WL", 320 * i, 320 * i + 320)
+
+    def wgath(out, k):
+        act(out, ind(r("WT", 0, 2064), r("WI", 20 * (k - 1), 20 * k)))
+
+    def sgath(lo, hi):
+        act(r("SG", (lo - 1) * 320, hi * 320), ind(r("S16", 0, 2320), r("HI", 20 * (lo - 1), 20 * hi)))
+
+    def stage(bank, *terms):
+        for i, (m, x) in enumerate(terms):
+            mm(r(bank, 0, 320), r(m, 0, 128), x, i == 0, i == len(terms) - 1, i == len(terms) - 1)
+
+    def pair_sum(bank, u):
+        stage(bank, ("ID", row("WU", u)), ("ID", lower(u - 1)))
+
+    def gap(bank, u):
+        stage(bank, ("NI", row("WU", u)), ("ID", row("SG", u)))
+
+    def plain(bank, k):
+        stage(bank, ("ID", row("SG", k)))
+
+    def chain(k):
+        up = r("IMP", 0, 320) if k == 11 else row("OWN", k + 1)
+        tt(row("OWN", k), ind(r("WT", 0, 2064), r("WI", 20 * (k - 1), 20 * k)), up, A.add)
+
+    def chain2(bank, u):
+        tt(row("OWN", u - 1), r(bank, 0, 320), row("OWN", u + 1), A.add)
+
+    def over(bank, k):
+        tt(r("OVER", k * 320, k * 320 + 320), r(bank, 0, 320), row("OWN", k + 1 if k in UPPER else k), A.is_lt)
+
+    def comp(k):
+        tt(r("OVER", k * 320, k * 320 + 320), ind(r("S16", 0, 2320), r("HI", 20 * (k - 1), 20 * k)), row("OWN", k), A.is_lt)
+
+    def votes(c):
+        k0, k1 = ((10, 12), (6, 10), (3, 6), (0, 3))[c]
+        kp = r("K%d" % c, 0, 20 * (k1 - k0))
+        mm(kp, r("ID", 0, 128), r("KK", 20 * k0, 20 * k1), True, False, False)
+        for j in range(16):
+            mm(kp, r("Z", 15 - j, 143 - j), r("OVER", k0 * 320 + j, k1 * 320, 16), False, j == 15, j == 15)
+
+    def strengths(lo, hi, frm):
+        act(r("S16", lo, hi), r("ST", frm, frm + hi - lo), F.Identity, -OFF, 16.0)
+
+    for t in range(RO):
+        last = t == RO - 1
+        ts(r("WI", 0, 220), r("C", 20, 240), 16.0, A.add)
+        act(r("POS", 0, 220), r("C", 0, 220), F.Identity, 32.0)
+        for u, bank in zip(UPPER, ("ACC", "EX", "TOT")):
+            wgath(row("WU", u), u)
+            wgath(lower(u - 1), u - 1)
+            pair_sum(bank, u)
+        tt(r("P", 0, 220), r("C", 20, 240), r("POS", 0, 220), A.mult)
+        if t > 0:
+            chain(11)
+        ts(r("Q", 0, 220), r("P", 0, 220), 5, A.arith_shift_right, 2047 | (1 << 20), A.bitwise_and)
+        if t > 0:
+            chain(10)
+        ts(r("HI", 0, 220), r("Q", 0, 220), 77.0 * t, A.add, 2304.0, A.min)
+        if t == 0:
+            act(r("Z", 15, 143, 16), r("BO", 0, 128, 16), F.Identity, 0.0, 97.0)
+            act(r("KK", 0, 240), r("KK", 0, 240), F.Identity, 0.0, 1.0 / 32)
+            strengths(0, 1024, 0)
+            strengths(2048, 2304, 0)
+            strengths(1024, 2048, 1024)
+            invert_targets(chain)
+            comp(11)
+            comp(10)
+        else:
+            comp(11)
+            chain(9)
+            comp(10)
+            chain(8)
+        votes(0)
+        sgath(6, 7)
+        gap("POS", 7)
+        plain("K3", 6)
+        sgath(4, 5)
+        sgath(2, 3)
+        comp(9)
+        chain2("ACC", 7)
+        comp(8)
+        chain2("EX", 5)
+        gap("K2", 5)
+        plain("ACC", 4)
+        over("POS", 7)
+        chain2("TOT", 3)
+        gap("EX", 3)
+        plain("TOT", 2)
+        over("K3", 6)
+        votes(1)
+        over("K2", 5)
+        over("ACC", 4)
+        over("EX", 3)
+        votes(2)
+        chain(1)
+        act(r("C13", 0, 240), r("C", 0, 240), F.Identity, float(t), 13.0)
+        act(r("KS", 200, 240), r("K0", 0, 40))
+        for u in UPPER:
+            act(row("OWN", u), row("OWN", u + 1))
+        if t == 0:
+            act(r("NH", 0, 128), r("ID", 0, 128), F.Identity, 0.0, -1.0)
+            act(r("IF", 0, 128), r("ID", 0, 128))
+            act(r("NB", 0, 128), r("BO", 0, 128), F.Identity, 0.0, -BIG)
+            pick(r("TR", 0, 128), r("NB", 0, 128), [[1, 128]], A.is_gt, 0, -1)
+            pick(r("TR", 0, 128), r("TR", 0, 128), [[1, 128]], A.not_equal, 0, -1, 80 * BIG)
+        act(r("KS", 120, 200), r("K1", 0, 80))
+        over("TOT", 2)
+        comp(1)
+        votes(3)
+        tt(r("TT", 120, 240), r("KS", 120, 240), r("C13", 120, 240), A.add)
+        tt(r("TT", 60, 120), r("K2", 0, 60), r("C13", 60, 120), A.add)
+        tt(r("M60", 0, 60), r("KS", 120, 180), r("KS", 180, 240), A.max)
+        ts(r("CN", 60, 240), r("TT", 60, 240), 2047, A.bitwise_and)
+        tt(r("M61", 0, 60), r("K2", 0, 60), r("M60", 0, 60), A.max)
+        cp(r("WB", 60, 240), r("CN", 60, 240))
+        act(r("B", 16, 336), ind(r("WB", 0, 240), r("LBU", 0, 20)))
+        built = ("a", count["a"])
+        tt(r("M60", 0, 20), r("M61", 0, 20), r("M61", 20, 40), A.max)
+        ts(sm(N1), r("NU", 0, 20), U, A.add, 12 * U, A.min)
+        tt(r("M60", 20, 40), r("M60", 0, 20), r("M61", 40, 60), A.max)
+        mm(r("TOT", 0, 20), r("ID", 0, 128), r("NEG", 0, 20), True, False, False)
+        tt(sm(KEY1), r("K3", 20, 40), r("M60", 20, 40), A.max)
+        tt(r("TT", 0, 60), r("K3", 0, 60), r("C13", 0, 60), A.add)
+        tt(r("KB", 0, 20), r("K3", 40, 60), sm(KEY1), A.max)
+        mm(r("TOT", 0, 20), r("GS", 0, 128), r("KB", 0, 20), False, True)
+        tt(sm(KEY), r("K3", 40, 60), sm(KEY1), A.max)
+        ts(r("CN", 0, 60), r("TT", 0, 60), 2047, A.bitwise_and)
+        cp(r("SI", 0, 20), sm(KEY))
+        ts(sm(THR), sm(KEY), 872.5, A.is_lt, 1.0e6, A.mult)
+        tt(sm(FR), sm(KEY), r("SI", 0, 20), A.subtract)
+        tt(r("RD", 0, 20), r("TOT", 0, 20), sm(THR), A.is_gt)
+        act(sm(A1), sm(FR), F.Identity, 3200.0, -10240.0)
+        act(r("B", 28, 336, 16), sm(FR), F.Identity, 11 * U, -32 * U, built)
+        ts(sm(KST), sm(FR), -32 * U, A.mult, 11 * U, A.add)
+        mm(r("POS", 0, 20), r("TR", 0, 128), r("RD", 0, 20), True, False, False)
+        emit("v", lambda: g.vector.tensor_tensor_scan(T.CUM[:, 1:21], T.ONE[:, 0:20], T.RD[:, 0:20], 0.0, A.mult, A.add),
+             [("ONE", 0, 20), ("RD", 0, 20)], [("CUM", 1, 21)])
+        mm(r("POS", 0, 20), r("NB", 0, 128), r("CUM", 0, 20), False, True)
+        tt(sm(A2), sm(A1), sm(SC), A.add)
+        tt(sm(LEN), r("NU", 0, 20), sm(KST), A.subtract)
+        cp(r("AL", 0, 20), sm(A2))
+        act(r("L1", 0, 320), ind(r("OWN", 0, 3520), r("AL", 0, 20)))
+        act(r("EX", 0, 220), r("GSC", 0, 220), F.Identity, float(997 * t - ((t - 13) & 2047)))
+        act(r("ACC", 0, 220), r("C", 20, 240), F.Relu, 0.0, -1.0)
+        cp(r("B", 17, 336, 16), r("CN", 20, 40), built)
+        cp(r("B", 18, 336, 16), r("CN", 40, 60), built)
+        tt(r("B", 30, 336, 16), r("POS", 0, 20), sm(S8), A.min, built)
+        tt(r("B", 29, 336, 16), r("POS", 0, 20), sm(LEN), A.min, built)
+        ts(sm(SL), r("POS", 0, 20), 0.0, A.is_gt)
+        tr(r("KW", 0, 320), r("B", 16, 336))
+        tr(r("KW", 320, 672), r("B", 0, 352))
+        act(r("MK%d" % t, 0, 160), ind(r("KW", 0, 672), r("PL", 0, 10)), F.Relu)
+        ts(r("MK%d" % t, 160, 320), ind(r("KW", 0, 672), r("PL", 10, 20)), 0.0, A.max)
+        send(t, "MK%d" % t, "RK%d" % t, "rk%d" % t)
+        act(r("L2", 0, 320), ind(r("WU", 0, 3520), r("AL", 0, 20)))
+        mm(r("K0", 0, 320), r("NH", 0, 128), r("IMP", 0, 320), True, False, False)
+        mm(r("K0", 0, 320), r("IF", 0, 128), r("L1", 0, 320), False, False, False)
+        mm(r("K0", 0, 320), r("ID", 0, 128), r("L2", 0, 320), False, True)
+        tt(sm(DK), sm(KST), sm(N1), A.subtract)
+        tt(r("G1", 0, 220), r("CN", 0, 220), r("EX", 0, 220), A.add)
+        tt(sm(DK), sm(DK), sm(SL), A.mult)
+        tt(r("G2", 0, 220), r("G1", 0, 220), r("ACC", 0, 220), A.mult)
+        tt(sm(N4), sm(DK), sm(N1), A.add)
+        cp(r("C", 0, 20), r("CN", 0, 20))
+        tt(r("V4", 0, 224), ind(sm(N4), r("LBC", 0, 14)), r("KU", 20, 244), A.subtract)
+        act(r("ML%d" % t, 8, 328), r("K0", 0, 320))
+        send(t, "ML%d" % t, "RL%d" % t, "rl%d" % t)
+        act(r("R1", 0, 220), r("V4", 0, 220), F.Relu, 1.0)
+        act(r("K3", 0, 224), r("V4", 0, 224), F.Relu, 0.0, 17.0)
+        act(r("K2", 0, 220), r("R1", 0, 220), F.Identity, -1.0)
+        tt(r("G3", 0, 220), r("G2", 0, 220), r("CN", 20, 240), A.add)
+        ts(r("G4", 0, 220), r("G3", 0, 220), 2047, A.bitwise_and)
+        tt(r("QQ", 0, 224), r("V4", 0, 224), r("K3", 0, 224), A.subtract)
+        tt(r("TOT", 0, 220), r("G4", 0, 220), r("K2", 0, 220), A.min)
+        arrival(t, "RK%d" % t, "rk%d" % t)
+        arrival(t, "RL%d" % t, "rl%d" % t)
+        tr(r("XT", 0, 320), r("RK%d" % t, 0, 320))
+        tt(sm(D0), r("XT", 12, 320, 16), sm(N4), A.subtract)
+        cp(sm(LS), r("XT", 13, 320, 16))
+        ts(sm(D1), sm(D0), 0.0, A.is_gt, -11 * U, A.mult)
+        cp(r("IL", 0, 20), r("XT", 14, 320, 16))
+        tt(sm(BETA), sm(D0), sm(D1), A.add)
+        for h in (0, 1):
+            tt(r("Y", 160 * h, 160 * h + 160), ind(sm(BETA), r("LY", 10 * h, 10 * h + 10)), r("XT", 160 * h, 160 * h + 160), A.add)
+        off = -15 * 2048.0
+        for s in range(5):
+            src, dst = ("O1", "O0") if s % 2 == 0 else ("O0", "O1")
+            for h in (0, 1):
+                ca = r("CA", 112 * h, 112 * h + 112)
+                out = r(dst, 112 * h, 112 * h + 112)
+                mirror = r("LBA", 8 * s + 8, 8 * s + 15)
+                if s == 0:
+                    win = r("Y", 160 * h, 160 * h + 160)
+                    act(ca, ind(win, mirror), F.Identity, 2 * off, -1.0)
+                    if h == 0:
+                        tt(r("V0", 0, 224), ind(sm(LS), r("LBC", 0, 14)), r("QQ", 0, 224), A.add)
+                    tt(out, ind(win, r("LBA", 0, 7)), ca, A.max)
+                else:
+                    win = r(src, 112 * h, 112 * h + 112)
+                    act(ca, win, F.Identity, 2 * off, -1.0)
+                    tt(out, ind(ca, mirror), win, A.max)
+            if s == 1:
+                tt(sm(TMP), sm(N4), sm(LS), A.add)
+            if s == 2:
+                ts(r("NU", 0, 20), sm(TMP), 12 * U, A.min)
+            if s == 3 and last:
+                ts(sm(TMP), r("NU", 0, 20), 1.0 / U, A.mult)
+                store("s", "d_yn", T.yn[:], sm(TMP))
+            off += 2048.0 * (8 >> s)
+        land = ind(r("RL%d" % t, 0, 328), r("IL", 0, 20))
+        if last:
+            act(r("YI", 0, 320), land)
+            store("a", "d_yi", T.yi[:], r("YI", 0, 320))
+        else:
+            act(r("IMP", 0, 320), land, F.Identity, -OFF)
+        tt(r("G1", 0, 224), ind(r("O0", 0, 224), r("LMG", 0, 14)), r("V0", 0, 224), A.min)
+        tt(r("C", 20, 240), r("G1", 0, 220), r("TOT", 0, 220), A.max)
+
+    store("s", "d_yc", T.yc[:], r("C", 0, 240))
+    for sem in ("d_yi", "d_yn", "d_yc"):
+        wait("s", sem, 16)
+    for q in ("v", "a", "t", "p"):
+        wait("s", q, count[q])
+    g.wait_ge(T.sem.sent, sent[0])

@@ -3,32 +3,32 @@ from concourse.mybir import AluOpType, ActivationFunctionType
 A = AluOpType
 F = ActivationFunctionType
 RO = 4
-UPPER = (7, 5, 3)
-U = 4096.0
-OFF = 1408.0
+OFF = 1792.0
 BIG = 65536.0
+U = 1.0 / 32
+CA = 24.0
+C0 = CA - 1.5 * U
 
 SCRATCH = {}
 for _dt, _bufs in (
         ("int32", dict(CS=240, NS=32, DS=32, P=224, Q=224, TT=240, CN=240, SI=64, G3=240, G4=240, X=128, X2=128, PC=8,
-                       JI=64, HJ=16)),
-        ("bfloat16", dict(WT=2064, ST=2048, S16=2320, WU=3520, WL=960, SG=3520, L2=320, OVER=3840, KB=32, RD=32, CUM=32,
-                          Z=144, ID=128, NI=128, GS=128, BO=128, TR=128, NB=128, KK=240, NEG=32, ONE=128)),
-        ("float16", dict(IMP=320, XT=320, NH=128)),
-        ("uint16", dict(WI=224, HI=224, AL=32, IL=32, PL=32, LBC=16, LMG=16, LBA=48, LBU=32, LY=32)),
-        ("float32", dict(C=256, NU=32, L1=320, OWN=3520, C13=240, KS=240, WB=240, M60=64, M61=64, SM=640, B=352, KW=672,
-                         Y=320, O0=224, O1=224, CA=224, G1=224, G2=224, V4=240, R1=224, QQ=224, V0=224, YI=320, PF=16,
-                         IF=128, KU=256, GSC=224, J=64, J1=64, J2=64, J3=64, J4=32, H=64))):
+                       HJ=16)),
+        ("bfloat16", dict(WT=2064, ST=2048, S16=2320, WU=3840, WL=1280, SG=2240, OVER=3840, KB=32, RD=32, CUM=32,
+                          Z=144, ID=128, NI=128, GS=128, BO=128, TR=128, NB=128, KK=240, NEG=32, ONE=128, AH=32)),
+        ("float16", dict(C=256, IMP=320, XT=320, O8=320, IH=128, NH=128, I16K=128, N16K=128, N4K=128, K32=224, ZH=224, XH=224,
+                         BB=224, UP=224, LM=224, Z0=224, Z1=224, Z2=224, Z3=224, Z4=224, Z5=224)),
+        ("uint16", dict(WI=224, HI=224, AL=32, INV=32, PL=32, LBC=16, LBU=32)),
+        ("float32", dict(CF=256, NU=32, OWN=3840, LA=320, LB=320, C13=240, KS=128, WB=240, M60=64, M61=64, SM=768,
+                         B=352, KW=672, Y=352, G1=224, V4=240, BASE=224, YI=320, PF=16, KU=256, KV=224, KF=224,
+                         GSC=224, Y1=224, J4=32, H=64))):
     for _n, _w in _bufs.items():
         SCRATCH[_n] = ("sbuf", [128, _w], _dt)
-PSUM = ("K0", "K1", "K2", "K3", "ACC", "TOT", "POS", "EX")
+PSUM = ("POS", "BX", "BY", "BZ", "K1", "K2", "K3", "TOT")
 for _n in PSUM:
     SCRATCH[_n] = ("psum", [128, 512], "float32")
 for _t in range(RO):
-    SCRATCH["MK%d" % _t] = ("sbuf", [128, 320], "float16")
-    SCRATCH["RK%d" % _t] = ("sbuf", [128, 320], "float16")
-    SCRATCH["ML%d" % _t] = ("sbuf", [128, 328], "float32")
-    SCRATCH["RL%d" % _t] = ("sbuf", [128, 328], "float32")
+    for _n in ("MK", "RK", "ML", "RL"):
+        SCRATCH["%s%d" % (_n, _t)] = ("sbuf", [128, 320], "float16")
 SEMAPHORES = (["v", "a", "t", "p", "sent", "d_cs", "d_ns", "d_ds", "d_wt", "d_s0", "d_s1", "d_yc", "d_yn", "d_yi"]
               + ["rk%d" % t for t in range(RO)] + ["rl%d" % t for t in range(RO)])
 
@@ -149,15 +149,15 @@ def rank_program(g, core, T, topo):
     def send(t, src, dst, sem):
         to = T.cores[(rank + 1 + t % (n_ranks - 1)) % n_ranks]
         rid, pid = topo.addr(to, core)
-        order("p", [(src, 0, 328)], [])
+        order("p", [(src, 0, 320)], [])
         g.remote_dma(T[dst][:], T[src][:], T.sem[sem], T.sem.sent, pid, rid, topo.mask(core, to))
         sent[0] += len(topo.engines(core, to))
 
     def arrival(t, name, sem):
         frm = T.cores[(rank - 1 - t % (n_ranks - 1)) % n_ranks]
-        log[name] = [(0, 328, True, sem, len(topo.engines(frm, core)))]
+        log[name] = [(0, 320, True, sem, len(topo.engines(frm, core)))]
 
-    (KEY1, KEY, THR, FR, SL, A1, A2, LEN, N1, DK, N4, D0, D1, BETA, LS, SC, S8, TMP, KST) = range(19)
+    (KEY, THR, FR, SL, A1, A2, NA, DK, NQ0, NQ, N4C, D, M, BETA, BQ, E2, SC, SC2, TMP, PM, T1, T2) = range(22)
 
     load("s", "d_cs", r("CS", 0, 240), T.cs[:])
     load("s", "d_ns", r("NS", 0, 20), T.ns[:])
@@ -168,327 +168,329 @@ def rank_program(g, core, T, topo):
 
     iota(r("PC", 0, 1), [[0, 1]], 0, 1, False)
     iota(r("H", 0, 16), [[16, 16]], 0)
-    iota(r("J", 0, 48), [[0, 6], [16, 8]], 0)
-    iota(r("KU", 0, 240), [[4096, 12], [0, 20]], 1)
-    iota(r("J4", 0, 20), [[1, 20]], 0)
-    iota(r("X", 0, 128), [[1, 128]], 0, 0, False)
-    fill(r("ONE", 0, 128), 1.0)
-    fill(r("WT", 0, 16), 0.0)
-    fill(r("IMP", 0, 320), -OFF)
-    pick(r("ID", 0, 128), r("ONE", 0, 128), [[-1, 128]], A.is_equal, 0, 1)
     iota(r("YI", 0, 320), [[32, 10], [1024, 2], [1, 16]], 0)
-    for k in range(1, 12):
-        if k not in UPPER:
-            act(r("WU", (k - 1) * 320, k * 320), r("IMP", 0, 320), F.Identity, 0.0, 0.0)
-    act(r("OVER", 0, 320), r("IMP", 0, 320), F.Identity, 0.0, 0.0)
+    iota(r("KU", 0, 240), [[4096, 12], [0, 20]], 1)
+    fill(r("ONE", 0, 128), 1.0)
+    fill(r("IMP", 0, 320), -OFF)
+    fill(r("WT", 0, 16), 0.0)
+    pick(r("ID", 0, 128), r("ONE", 0, 128), [[-1, 128]], A.is_equal, 0, 1)
+    iota(r("J4", 0, 20), [[1, 20]], 0)
+    act(r("K32", 0, 224), r("IMP", 0, 224), F.Identity, 32.0, 0.0)
     act(r("Z", 0, 144), r("IMP", 0, 144), F.Identity, 0.0, 0.0)
+    act(r("OVER", 0, 320), r("IMP", 0, 320), F.Identity, 0.0, 0.0)
+    act(r("Y", 0, 16), r("IMP", 0, 16), F.Identity, 0.0, 0.0)
+    act(r("Y", 336, 352), r("IMP", 0, 16), F.Identity, 0.0, 0.0)
+    act(r("IH", 0, 128), r("ID", 0, 128))
+    act(r("NI", 0, 128), r("ID", 0, 128), F.Identity, 0.0, -1.0)
     act(r("NEG", 0, 32), r("IMP", 0, 32), F.Identity, -7328.0, 0.0)
     act(r("CUM", 0, 32), r("IMP", 0, 32), F.Identity, 0.0, 0.0)
-    act(r("NI", 0, 128), r("ID", 0, 128), F.Identity, 0.0, -1.0)
+    act(r("OWN", 3520, 3840), r("IMP", 0, 320))
+    for k in (2, 4, 6, 8, 9, 10, 11, 12):
+        act(r("WU", (k - 1) * 320, k * 320), r("IMP", 0, 320), F.Identity, 0.0, 0.0)
     pick(r("BO", 0, 128), r("ONE", 0, 128), [[-16, 8], [0, 16]], A.is_ge, 0, 1)
     pick(r("BO", 0, 128), r("BO", 0, 128), [[16, 8], [0, 16]], A.is_ge, 15, -1)
     iota(r("KK", 0, 240), [[-1, 12], [0, 20]], 11)
+    iota(r("X", 0, 128), [[1, 128]], 0, 0, False)
+    iota(sm(PM), [[0, 10], [16, 2]], 0)
     iota(r("GSC", 0, 220), [[0, 11], [496, 20]], 0)
-    iota(r("KU", 240, 244), [[0, 4]], 0)
+    iota(r("KV", 0, 220), [[1, 11], [0, 20]], -10)
+    iota(r("KV", 220, 224), [[0, 4]], 0)
     iota(r("WB", 0, 60), [[0, 60]], 0)
     iota(r("B", 0, 16), [[0, 16]], 0)
     iota(r("B", 336, 352), [[0, 16]], 0)
-    for t in range(RO):
-        iota(r("ML%d" % t, 0, 8), [[0, 8]], 0)
 
     ts(r("PC", 1, 2), r("PC", 0, 1), 15, A.bitwise_and)
     ts(r("PC", 2, 3), r("PC", 0, 1), 16, A.bitwise_and)
     fill(r("S16", 2304, 2320), 1.0e6)
     cp(r("PF", 0, 3), r("PC", 0, 3))
     rc = r("PF", 1, 2)
-    for i, q in enumerate((0, -15, -7, -3, -1, 0)):
-        fill(r("J1", 8 * i, 8 * i + 8), float((q - 2) % 11))
-        if i == 0:
-            ts(r("H", 0, 16), r("H", 0, 16), rc, A.add)
-        if i == 1:
-            ts(r("J", 0, 48), r("J", 0, 48), rc, A.add)
-        if i == 2:
-            ts(r("HJ", 0, 16), r("H", 0, 16), -9.5, A.add, 0.05, A.mult)
-        if i == 3:
-            ts(r("JI", 0, 48), r("J", 0, 48), -4.5, A.add, 0.1, A.mult)
-        if i == 4:
-            ts(r("H", 16, 32), r("HJ", 0, 16), -20.0, A.mult)
-    ts(r("J2", 0, 48), r("JI", 0, 48), -10.0, A.mult)
-    tt(r("H", 32, 48), r("H", 16, 32), r("H", 0, 16), A.add)
-    tt(r("J1", 0, 48), r("J1", 0, 48), r("JI", 0, 48), A.subtract)
-    cp(r("LBC", 0, 16), r("H", 32, 48))
-    tt(r("J2", 0, 48), r("J2", 0, 48), r("J", 0, 48), A.add)
-    ts(r("J3", 0, 48), r("J1", 0, 48), 0.0, A.is_lt, 11.0, A.mult)
-    ts(r("H", 48, 64), r("H", 32, 48), 9.5, A.is_gt, 102.0, A.mult)
-    tt(r("J1", 0, 48), r("J1", 0, 48), r("J3", 0, 48), A.add)
-    ts(r("H", 16, 32), r("HJ", 0, 16), 10.0, A.mult)
-    cp(r("J1", 0, 8), r("JI", 0, 8))
-    tt(r("H", 48, 64), r("H", 48, 64), r("H", 32, 48), A.add)
-    ts(r("J2", 0, 16), r("J2", 0, 16), 16.0, A.mult, 1.0, A.add)
-    ts(r("J1", 16, 48), r("J1", 16, 48), 10.0, A.mult)
-    tt(r("H", 48, 64), r("H", 48, 64), r("H", 16, 32), A.add)
-    ts(r("PF", 4, 5), rc, 31.0, A.mult)
-    tt(r("J1", 0, 48), r("J1", 0, 48), r("J2", 0, 48), A.add)
-    ts(r("LMG", 0, 16), r("H", 48, 64), 223.0, A.min)
+    ts(r("H", 0, 16), r("H", 0, 16), rc, A.add)
     ts(r("PF", 5, 6), rc, 11.0, A.min, 20.0, A.mult)
-    ts(r("LBA", 0, 16), r("J1", 0, 16), 159.0, A.min)
-    ts(r("LBA", 16, 48), r("J1", 16, 48), 111.0, A.min)
+    ts(r("HJ", 0, 16), r("H", 0, 16), -9.5, A.add, 0.05, A.mult)
     ts(r("PF", 6, 7), r("PF", 2, 3), 64.0, A.mult)
+    ts(r("H", 16, 32), r("HJ", 0, 16), -20.0, A.mult)
     ts(r("PF", 7, 8), r("PF", 2, 3), -2.0, A.mult, 352.0, A.add)
-    ts(r("LBU", 0, 20), r("J4", 0, 20), r("PF", 5, 6), A.add)
-    cp(r("LY", 0, 20), r("J4", 0, 20))
-    ts(sm(SC), r("J4", 0, 20), 16.0, A.mult, rc, A.add)
+    tt(r("H", 32, 48), r("H", 16, 32), r("H", 0, 16), A.add)
+    ts(r("PF", 4, 5), rc, 31.0, A.mult)
+    cp(r("LBC", 0, 16), r("H", 32, 48))
+    cp(r("AL", 0, 20), r("DS", 0, 20))
+    ts(sm(TMP), r("NS", 0, 20), 4096.0, A.mult)
+    emit("v", lambda: g.vector.tensor_copy(ind(r("Y", 16, 336), r("AL", 0, 20))[0], T.YI[:, 0:320]),
+         [("YI", 0, 320), ("AL", 0, 20)], [("Y", 16, 336)])
+    tt(r("V4", 0, 240), ind(sm(TMP), r("LBC", 0, 15)), r("KU", 0, 240), A.subtract)
     ts(r("NU", 0, 20), r("NS", 0, 20), U, A.mult)
-    ts(sm(S8), sm(SC), 8.0, A.add)
-    tt(r("V4", 0, 240), ind(r("NU", 0, 20), r("LBC", 0, 15)), r("KU", 0, 240), A.subtract)
-    ts(r("X2", 0, 128), r("X", 0, 128), 15, A.bitwise_and)
     tt(r("V4", 0, 240), r("V4", 0, 240), r("CS", 0, 240), A.min)
-    ts(r("GS", 0, 128), r("X2", 0, 128), rc, A.is_equal)
+    ts(sm(SC), r("J4", 0, 20), 16.0, A.mult, rc, A.add)
     ts(r("C", 0, 240), r("V4", 0, 240), -1.0, A.max)
 
-    def invert_targets(chain):
-        cp(r("AL", 0, 20), r("DS", 0, 20))
-        chain(11)
-        sc = ind(r("Y", 0, 320), r("AL", 0, 20))
-        emit("v", lambda: g.vector.tensor_copy(sc[0], T.YI[:, 0:320]), [("YI", 0, 320), ("AL", 0, 20)], [("Y", 0, 320)])
-        chain(10)
-        tr(r("KW", 0, 320), r("Y", 0, 320))
-        ts(r("GSC", 0, 220), r("GSC", 0, 220), r("PF", 4, 5), A.add)
+    def run_list():
+        tr(r("KW", 0, 320), r("Y", 16, 336))
+        ts(r("LBU", 0, 20), r("J4", 0, 20), r("PF", 5, 6), A.add)
         cp(r("SI", 0, 20), r("KW", 0, 320, 16))
-        chain(9)
+        cp(sm(T2), r("KW", 0, 320, 16))
+        chain(8)
         ts(r("SI", 20, 40), r("SI", 0, 20), 1024, A.bitwise_and)
         ts(r("SI", 40, 60), r("SI", 0, 20), 1023, A.bitwise_and)
+        ts(r("X2", 0, 128), r("X", 0, 128), 15, A.bitwise_and)
         ts(sm(A1), r("SI", 20, 40), r("PF", 6, 7), A.not_equal, r("PF", 7, 8), A.mult)
         ts(r("SI", 41, 60, 2), r("SI", 41, 60, 2), 16.0, A.add)
-        chain(8)
+        ts(r("GS", 0, 128), r("X2", 0, 128), rc, A.is_equal)
         tt(sm(A2), sm(A1), r("SI", 40, 60), A.add)
+        strengths(0, 1024, 0)
         cp(r("PL", 0, 20), sm(A2))
+
+    def load_list():
+        tr(r("KW", 320, 672), r("Y", 0, 352))
+        ts(sm(PM), sm(PM), r("PF", 2, 3), A.not_equal)
+        tt(sm(T1), r("KW", 336, 656, 16), sm(T2), A.subtract)
+        ts(r("GSC", 0, 220), r("GSC", 0, 220), r("PF", 4, 5), A.add)
+        tt(sm(T1), sm(T1), sm(PM), A.mult)
+        ts(sm(SC2), sm(SC), 3520.0, A.add)
+        tt(sm(T1), sm(T1), sm(T2), A.add)
+        ts(sm(T2), sm(T1), 1023.5, A.is_gt, -1008.0, A.mult)
+        tt(sm(T1), sm(T1), sm(T2), A.add)
+        cp(r("INV", 0, 20), sm(T1))
 
     def row(name, k):
         return r(name, (k - 1) * 320, k * 320)
 
-    def lower(k):
-        i = UPPER.index(k + 1)
-        return r("WL", 320 * i, 320 * i + 320)
+    def wrow(k):
+        return row("WU", k) if k % 2 else row("WL", k // 2)
 
-    def wgath(out, k):
-        act(out, ind(r("WT", 0, 2064), r("WI", 20 * (k - 1), 20 * k)))
+    def wgath(k):
+        act(wrow(k), ind(r("WT", 0, 2064), r("WI", 20 * (k - 1), 20 * k)))
 
     def sgath(lo, hi):
         act(r("SG", (lo - 1) * 320, hi * 320), ind(r("S16", 0, 2320), r("HI", 20 * (lo - 1), 20 * hi)))
 
-    def stage(bank, *terms):
-        for i, (m, x) in enumerate(terms):
-            mm(r(bank, 0, 320), r(m, 0, 128), x, i == 0, i == len(terms) - 1, i == len(terms) - 1)
+    SUMS = {7: "BY", 6: "BX", 4: "BZ"}
+    GAPS = {5: "TOT", 3: "POS", 1: "K3"}
 
-    def pair_sum(bank, u):
-        stage(bank, ("ID", row("WU", u)), ("ID", lower(u - 1)))
+    def weigh(k):
+        for j in sorted(SUMS, reverse=True):
+            if j <= k:
+                mm(r(SUMS[j], 0, 320), r("ID", 0, 128), wrow(k), k == 7, False, False)
+        if k in (3, 2):
+            mm(r("K2", 0, 320), r("ID", 0, 128), wrow(k), k == 3, k == 2, k == 2)
+        if k in GAPS:
+            mm(r(GAPS[k], 0, 320), r("NI", 0, 128), wrow(k), True, False, False)
 
-    def gap(bank, u):
-        stage(bank, ("NI", row("WU", u)), ("ID", row("SG", u)))
+    def base(j):
+        mm(r(SUMS[j], 0, 320), r("IH", 0, 128), r("O8", 0, 320), False, True)
 
-    def plain(bank, k):
-        stage(bank, ("ID", row("SG", k)))
+    def gap(k):
+        mm(r(GAPS[k], 0, 320), r("ID", 0, 128), row("SG", k), False, True)
 
-    def chain(k):
-        up = r("IMP", 0, 320) if k == 11 else row("OWN", k + 1)
-        tt(row("OWN", k), ind(r("WT", 0, 2064), r("WI", 20 * (k - 1), 20 * k)), up, A.add)
+    def own(k):
+        return r("O8", 0, 320) if k == 8 else row("OWN", k)
 
-    def chain2(bank, u):
-        tt(row("OWN", u - 1), r(bank, 0, 320), row("OWN", u + 1), A.add)
+    def chain(k, imp=None):
+        tt(own(k), ind(r("WT", 0, 2064), r("WI", 20 * (k - 1), 20 * k)), imp or own(k + 1), A.add)
 
-    def over(bank, k):
-        tt(r("OVER", k * 320, k * 320 + 320), r(bank, 0, 320), row("OWN", k + 1 if k in UPPER else k), A.is_lt)
+    def over(k):
+        if k in GAPS:
+            tt(r("OVER", k * 320, k * 320 + 320), r(GAPS[k], 0, 320), own(k + 1), A.is_lt)
+        else:
+            tt(r("OVER", k * 320, k * 320 + 320), row("SG", k), r(SUMS[k], 0, 320), A.is_lt)
 
     def comp(k):
-        tt(r("OVER", k * 320, k * 320 + 320), ind(r("S16", 0, 2320), r("HI", 20 * (k - 1), 20 * k)), row("OWN", k), A.is_lt)
+        tt(r("OVER", k * 320, k * 320 + 320), ind(r("S16", 0, 2320), r("HI", 20 * (k - 1), 20 * k)), own(k), A.is_lt)
 
-    def votes(c):
-        k0, k1 = ((10, 12), (6, 10), (3, 6), (0, 3))[c]
-        kp = r("K%d" % c, 0, 20 * (k1 - k0))
-        mm(kp, r("ID", 0, 128), r("KK", 20 * k0, 20 * k1), True, False, False)
+    def votes(bank, at, k0):
+        kp = r(bank, at, at + 60)
+        mm(kp, r("ID", 0, 128), r("KK", 20 * k0, 20 * k0 + 60), True, False, False)
         for j in range(16):
-            mm(kp, r("Z", 15 - j, 143 - j), r("OVER", k0 * 320 + j, k1 * 320, 16), False, j == 15, j == 15)
+            mm(kp, r("Z", 15 - j, 143 - j), r("OVER", k0 * 320 + j, (k0 + 3) * 320, 16), False, j == 15, j == 15)
 
     def strengths(lo, hi, frm):
-        act(r("S16", lo, hi), r("ST", frm, frm + hi - lo), F.Identity, -OFF, 16.0)
+        ts(r("S16", lo, hi), r("ST", frm, frm + hi - lo), 16.0, A.mult, -OFF, A.add)
+
+    def turn(bank, z, s, lhs="IH"):
+        mm(r(bank, 20 * s, 220), r(lhs, 0, 128), r(z, 0, 220 - 20 * s), False, s == 0, s == 0)
+        if s:
+            mm(r(bank, 0, 20 * s), r(lhs, 0, 128), r(z, 220 - 20 * s, 220), False, False, False)
 
     for t in range(RO):
         last = t == RO - 1
+        imp = r("IMP", 0, 320) if t == 0 else r("RL%d" % (t - 1), 0, 320)
         ts(r("WI", 0, 220), r("C", 20, 240), 16.0, A.add)
-        act(r("POS", 0, 220), r("C", 0, 220), F.Identity, 32.0)
-        for u, bank in zip(UPPER, ("ACC", "EX", "TOT")):
-            wgath(row("WU", u), u)
-            wgath(lower(u - 1), u - 1)
-            pair_sum(bank, u)
+        mm(r("POS", 0, 220), r("IH", 0, 128), r("K32", 0, 220), True, False, False)
+        mm(r("POS", 0, 220), r("IH", 0, 128), r("C", 0, 220), False, True)
+        for k in range(7, 0, -1):
+            wgath(k)
+        chain(11, imp)
         tt(r("P", 0, 220), r("C", 20, 240), r("POS", 0, 220), A.mult)
-        if t > 0:
-            chain(11)
+        chain(10)
         ts(r("Q", 0, 220), r("P", 0, 220), 5, A.arith_shift_right, 2047 | (1 << 20), A.bitwise_and)
-        if t > 0:
-            chain(10)
+        chain(9)
         ts(r("HI", 0, 220), r("Q", 0, 220), 77.0 * t, A.add, 2304.0, A.min)
         if t == 0:
+            run_list()
+            act(r("S16", 1024, 2048), r("ST", 1024, 2048), F.Identity, -OFF, 16.0)
             act(r("Z", 15, 143, 16), r("BO", 0, 128, 16), F.Identity, 0.0, 97.0)
-            act(r("KK", 0, 240), r("KK", 0, 240), F.Identity, 0.0, 1.0 / 32)
-            strengths(0, 1024, 0)
+            act(r("KK", 0, 240), r("KK", 0, 240), F.Identity, 0.0, U)
             strengths(2048, 2304, 0)
-            strengths(1024, 2048, 1024)
-            invert_targets(chain)
-            comp(11)
-            comp(10)
         else:
-            comp(11)
-            chain(9)
-            comp(10)
             chain(8)
-        votes(0)
-        sgath(6, 7)
-        gap("POS", 7)
-        plain("K3", 6)
-        sgath(4, 5)
-        sgath(2, 3)
+        for k in (7, 6, 5, 4):
+            weigh(k)
+        for j in (7, 6, 4):
+            base(j)
+        for k in (3, 2, 1):
+            weigh(k)
+        comp(11)
+        comp(10)
         comp(9)
-        chain2("ACC", 7)
+        votes("K1", 120, 9)
+        sgath(7, 7)
+        act(row("OWN", 6), r("BX", 0, 320))
+        sgath(5, 5)
+        gap(5)
+        act(row("OWN", 4), r("BZ", 0, 320))
+        sgath(3, 3)
+        sgath(2, 2)
+        sgath(1, 1)
         comp(8)
-        chain2("EX", 5)
-        gap("K2", 5)
-        plain("ACC", 4)
-        over("POS", 7)
-        chain2("TOT", 3)
-        gap("EX", 3)
-        plain("TOT", 2)
-        over("K3", 6)
-        votes(1)
-        over("K2", 5)
-        over("ACC", 4)
-        over("EX", 3)
-        votes(2)
-        chain(1)
+        over(7)
+        comp(6)
+        gap(3)
+        votes("K1", 60, 6)
+        over(5)
+        comp(4)
+        mm(r("BX", 0, 320), r("ID", 0, 128), row("SG", 2), True, True)
+        gap(1)
+        over(3)
+        votes("BZ", 0, 3)
+        tt(row("OWN", 2), r("K2", 0, 320), row("OWN", 4), A.add)
+        act(r("KS", 60, 120), r("K1", 120, 180))
         act(r("C13", 0, 240), r("C", 0, 240), F.Identity, float(t), 13.0)
-        act(r("KS", 200, 240), r("K0", 0, 40))
-        for u in UPPER:
-            act(row("OWN", u), row("OWN", u + 1))
+        tt(r("OVER", 640, 960), r("BX", 0, 320), row("OWN", 2), A.is_lt)
+        over(1)
+        votes("BY", 0, 0)
         if t == 0:
-            act(r("NH", 0, 128), r("ID", 0, 128), F.Identity, 0.0, -1.0)
-            act(r("IF", 0, 128), r("ID", 0, 128))
             act(r("NB", 0, 128), r("BO", 0, 128), F.Identity, 0.0, -BIG)
             pick(r("TR", 0, 128), r("NB", 0, 128), [[1, 128]], A.is_gt, 0, -1)
             pick(r("TR", 0, 128), r("TR", 0, 128), [[1, 128]], A.not_equal, 0, -1, 80 * BIG)
-        act(r("KS", 120, 200), r("K1", 0, 80))
-        over("TOT", 2)
-        comp(1)
-        votes(3)
-        tt(r("TT", 120, 240), r("KS", 120, 240), r("C13", 120, 240), A.add)
-        tt(r("TT", 60, 120), r("K2", 0, 60), r("C13", 60, 120), A.add)
-        tt(r("M60", 0, 60), r("KS", 120, 180), r("KS", 180, 240), A.max)
+        tt(r("M60", 0, 60), r("K1", 60, 120), r("KS", 60, 120), A.max)
+        tt(r("TT", 120, 240), r("K1", 60, 180), r("C13", 120, 240), A.add)
+        tt(r("TT", 60, 120), r("BZ", 0, 60), r("C13", 60, 120), A.add)
+        tt(r("M61", 0, 60), r("BZ", 0, 60), r("M60", 0, 60), A.max)
         ts(r("CN", 60, 240), r("TT", 60, 240), 2047, A.bitwise_and)
-        tt(r("M61", 0, 60), r("K2", 0, 60), r("M60", 0, 60), A.max)
+        tt(r("M61", 20, 40), r("M61", 0, 20), r("M61", 20, 40), A.max)
         cp(r("WB", 60, 240), r("CN", 60, 240))
+        act(row("OWN", 7), r("O8", 0, 320))
         act(r("B", 16, 336), ind(r("WB", 0, 240), r("LBU", 0, 20)))
         built = ("a", count["a"])
-        tt(r("M60", 0, 20), r("M61", 0, 20), r("M61", 20, 40), A.max)
-        ts(sm(N1), r("NU", 0, 20), U, A.add, 12 * U, A.min)
-        tt(r("M60", 20, 40), r("M60", 0, 20), r("M61", 40, 60), A.max)
         mm(r("TOT", 0, 20), r("ID", 0, 128), r("NEG", 0, 20), True, False, False)
-        tt(sm(KEY1), r("K3", 20, 40), r("M60", 20, 40), A.max)
-        tt(r("TT", 0, 60), r("K3", 0, 60), r("C13", 0, 60), A.add)
-        tt(r("KB", 0, 20), r("K3", 40, 60), sm(KEY1), A.max)
+        tt(r("M60", 0, 40), r("BY", 20, 60), r("M61", 20, 60), A.max)
+        tt(r("TT", 0, 60), r("BY", 0, 60), r("C13", 0, 60), A.add)
+        tt(r("KB", 0, 20), r("M60", 0, 20), r("M60", 20, 40), A.max)
         mm(r("TOT", 0, 20), r("GS", 0, 128), r("KB", 0, 20), False, True)
-        tt(sm(KEY), r("K3", 40, 60), sm(KEY1), A.max)
+        tt(sm(KEY), r("M60", 0, 20), r("M60", 20, 40), A.max)
         ts(r("CN", 0, 60), r("TT", 0, 60), 2047, A.bitwise_and)
-        cp(r("SI", 0, 20), sm(KEY))
         ts(sm(THR), sm(KEY), 872.5, A.is_lt, 1.0e6, A.mult)
-        tt(sm(FR), sm(KEY), r("SI", 0, 20), A.subtract)
+        cp(r("SI", 0, 20), sm(KEY))
         tt(r("RD", 0, 20), r("TOT", 0, 20), sm(THR), A.is_gt)
-        act(sm(A1), sm(FR), F.Identity, 3200.0, -10240.0)
-        act(r("B", 28, 336, 16), sm(FR), F.Identity, 11 * U, -32 * U, built)
-        ts(sm(KST), sm(FR), -32 * U, A.mult, 11 * U, A.add)
+        tt(sm(FR), sm(KEY), r("SI", 0, 20), A.subtract)
         mm(r("POS", 0, 20), r("TR", 0, 128), r("RD", 0, 20), True, False, False)
         emit("v", lambda: g.vector.tensor_tensor_scan(T.CUM[:, 1:21], T.ONE[:, 0:20], T.RD[:, 0:20], 0.0, A.mult, A.add),
              [("ONE", 0, 20), ("RD", 0, 20)], [("CUM", 1, 21)])
         mm(r("POS", 0, 20), r("NB", 0, 128), r("CUM", 0, 20), False, True)
-        tt(sm(A2), sm(A1), sm(SC), A.add)
-        tt(sm(LEN), r("NU", 0, 20), sm(KST), A.subtract)
-        cp(r("AL", 0, 20), sm(A2))
-        act(r("L1", 0, 320), ind(r("OWN", 0, 3520), r("AL", 0, 20)))
-        act(r("EX", 0, 220), r("GSC", 0, 220), F.Identity, float(997 * t - ((t - 13) & 2047)))
-        act(r("ACC", 0, 220), r("C", 20, 240), F.Relu, 0.0, -1.0)
+        act(r("B", 28, 336, 16), sm(FR), F.Identity, 0.0, 1.0, built)
+        act(row("OWN", 1), row("OWN", 2))
         cp(r("B", 17, 336, 16), r("CN", 20, 40), built)
         cp(r("B", 18, 336, 16), r("CN", 40, 60), built)
-        tt(r("B", 30, 336, 16), r("POS", 0, 20), sm(S8), A.min, built)
-        tt(r("B", 29, 336, 16), r("POS", 0, 20), sm(LEN), A.min, built)
-        ts(sm(SL), r("POS", 0, 20), 0.0, A.is_gt)
+        tt(r("B", 29, 336, 16), r("POS", 0, 20), r("NU", 0, 20), A.min, built)
         tr(r("KW", 0, 320), r("B", 16, 336))
         tr(r("KW", 320, 672), r("B", 0, 352))
+        act(row("OWN", 3), row("OWN", 4))
         act(r("MK%d" % t, 0, 160), ind(r("KW", 0, 672), r("PL", 0, 10)), F.Relu)
         ts(r("MK%d" % t, 160, 320), ind(r("KW", 0, 672), r("PL", 10, 20)), 0.0, A.max)
         send(t, "MK%d" % t, "RK%d" % t, "rk%d" % t)
-        act(r("L2", 0, 320), ind(r("WU", 0, 3520), r("AL", 0, 20)))
-        mm(r("K0", 0, 320), r("NH", 0, 128), r("IMP", 0, 320), True, False, False)
-        mm(r("K0", 0, 320), r("IF", 0, 128), r("L1", 0, 320), False, False, False)
-        mm(r("K0", 0, 320), r("ID", 0, 128), r("L2", 0, 320), False, True)
-        tt(sm(DK), sm(KST), sm(N1), A.subtract)
-        tt(r("G1", 0, 220), r("CN", 0, 220), r("EX", 0, 220), A.add)
+        if t == 0:
+            load_list()
+        act(row("OWN", 5), row("OWN", 6))
+        act(row("OWN", 8), r("O8", 0, 320))
+        ts(sm(SL), r("POS", 0, 20), 0.0, A.is_gt)
+        ts(sm(A1), sm(FR), U, A.add, -10240.0, A.mult)
+        ts(sm(NA), r("NU", 0, 20), -10 * U, A.add, U, A.min)
+        tt(sm(A1), sm(A1), sm(SL), A.mult)
+        tt(sm(DK), sm(FR), sm(NA), A.add)
+        tt(sm(A2), sm(A1), sm(SC2), A.add)
         tt(sm(DK), sm(DK), sm(SL), A.mult)
-        tt(r("G2", 0, 220), r("G1", 0, 220), r("ACC", 0, 220), A.mult)
-        tt(sm(N4), sm(DK), sm(N1), A.add)
-        cp(r("C", 0, 20), r("CN", 0, 20))
-        tt(r("V4", 0, 224), ind(sm(N4), r("LBC", 0, 14)), r("KU", 20, 244), A.subtract)
-        act(r("ML%d" % t, 8, 328), r("K0", 0, 320))
+        cp(r("AL", 0, 20), sm(A2))
+        tt(sm(NQ0), sm(NA), sm(DK), A.subtract)
+        act(r("BY", 0, 220), r("GSC", 0, 220), F.Identity, float(997 * t - ((t - 13) & 2047)))
+        act(r("TOT", 0, 220), r("C", 20, 240), F.Relu, 0.0, -1.0)
+        if t == 0:
+            act(r("KF", 0, 224), r("KV", 0, 224), F.Identity, 11 * U + C0, U)
+            act(r("KV", 0, 224), r("KV", 0, 224), F.Identity, 0.0, U)
+            act(r("ZH", 0, 224), r("K32", 0, 224), F.Identity, 0.0, 0.0)
+            act(r("NH", 0, 128), r("ID", 0, 128), F.Identity, 0.0, -1.0)
+            act(r("I16K", 0, 128), r("ID", 0, 128), F.Identity, 0.0, 16384.0)
+            act(r("N16K", 0, 128), r("ID", 0, 128), F.Identity, 0.0, -16384.0)
+            act(r("N4K", 0, 128), r("ID", 0, 128), F.Identity, 0.0, -4096.0)
+            act(r("XH", 220, 224), r("K32", 0, 4), F.Identity, 0.0, 0.0)
+        tt(r("LA", 0, 320), ind(r("OWN", 0, 3840), r("AL", 0, 20)), imp, A.subtract)
+        ts(sm(NQ), sm(NQ0), C0, A.add)
+        tt(r("LB", 0, 320), ind(r("WU", 0, 3840), r("AL", 0, 20)), r("LA", 0, 320), A.add)
+        act(r("ML%d" % t, 0, 320), ind(r("LB", 0, 320), r("INV", 0, 20)), F.Identity, -OFF)
         send(t, "ML%d" % t, "RL%d" % t, "rl%d" % t)
-        act(r("R1", 0, 220), r("V4", 0, 220), F.Relu, 1.0)
-        act(r("K3", 0, 224), r("V4", 0, 224), F.Relu, 0.0, 17.0)
-        act(r("K2", 0, 220), r("R1", 0, 220), F.Identity, -1.0)
-        tt(r("G3", 0, 220), r("G2", 0, 220), r("CN", 20, 240), A.add)
-        ts(r("G4", 0, 220), r("G3", 0, 220), 2047, A.bitwise_and)
-        tt(r("QQ", 0, 224), r("V4", 0, 224), r("K3", 0, 224), A.subtract)
-        tt(r("TOT", 0, 220), r("G4", 0, 220), r("K2", 0, 220), A.min)
+        tt(r("V4", 0, 224), ind(sm(NQ0), r("LBC", 0, 14)), r("KV", 0, 224), A.subtract)
+        tt(r("G1", 0, 220), r("CN", 0, 220), r("BY", 0, 220), A.add)
+        act(r("LM", 0, 220), r("V4", 0, 220), F.Relu, 0.0, 32.0)
+        act(r("K1", 0, 220), r("LM", 0, 220), F.Identity, -1.0, 4096.0)
+        cp(r("CF" if last else "C", 0, 20), r("CN", 0, 20))
+        tt(r("K2", 0, 220), r("G1", 0, 220), r("TOT", 0, 220), A.mult)
+        ts(sm(N4C), sm(NQ0), C0 + 11 * U, A.add)
+        tt(r("G3", 0, 220), r("K2", 0, 220), r("CN", 20, 240), A.add)
+        mm(r("BX", 0, 220), r("IH", 0, 128), r("ZH", 0, 220), True, False, False)
+        mm(r("BZ", 0, 220), r("IH", 0, 128), r("ZH", 0, 220), True, False, False)
+        mm(r("K3", 0, 220), r("N4K", 0, 128), r("LM", 0, 220), True, False)
         arrival(t, "RK%d" % t, "rk%d" % t)
         arrival(t, "RL%d" % t, "rl%d" % t)
         tr(r("XT", 0, 320), r("RK%d" % t, 0, 320))
-        tt(sm(D0), r("XT", 12, 320, 16), sm(N4), A.subtract)
-        cp(sm(LS), r("XT", 13, 320, 16))
-        ts(sm(D1), sm(D0), 0.0, A.is_gt, -11 * U, A.mult)
-        cp(r("IL", 0, 20), r("XT", 14, 320, 16))
-        tt(sm(BETA), sm(D0), sm(D1), A.add)
-        for h in (0, 1):
-            tt(r("Y", 160 * h, 160 * h + 160), ind(sm(BETA), r("LY", 10 * h, 10 * h + 10)), r("XT", 160 * h, 160 * h + 160), A.add)
-        off = -15 * 2048.0
-        for s in range(5):
-            src, dst = ("O1", "O0") if s % 2 == 0 else ("O0", "O1")
-            for h in (0, 1):
-                ca = r("CA", 112 * h, 112 * h + 112)
-                out = r(dst, 112 * h, 112 * h + 112)
-                mirror = r("LBA", 8 * s + 8, 8 * s + 15)
-                if s == 0:
-                    win = r("Y", 160 * h, 160 * h + 160)
-                    act(ca, ind(win, mirror), F.Identity, 2 * off, -1.0)
-                    if h == 0:
-                        tt(r("V0", 0, 224), ind(sm(LS), r("LBC", 0, 14)), r("QQ", 0, 224), A.add)
-                    tt(out, ind(win, r("LBA", 0, 7)), ca, A.max)
-                else:
-                    win = r(src, 112 * h, 112 * h + 112)
-                    act(ca, win, F.Identity, 2 * off, -1.0)
-                    tt(out, ind(ca, mirror), win, A.max)
-            if s == 1:
-                tt(sm(TMP), sm(N4), sm(LS), A.add)
-            if s == 2:
-                ts(r("NU", 0, 20), sm(TMP), 12 * U, A.min)
-            if s == 3 and last:
-                ts(sm(TMP), r("NU", 0, 20), 1.0 / U, A.mult)
-                store("s", "d_yn", T.yn[:], sm(TMP))
-            off += 2048.0 * (8 >> s)
-        land = ind(r("RL%d" % t, 0, 328), r("IL", 0, 20))
-        if last:
-            act(r("YI", 0, 320), land)
-            store("a", "d_yi", T.yi[:], r("YI", 0, 320))
+        for k in range(1, 12):
+            mm(r("BX", 20 * k - 20, 20 * k), r("IH", 0, 128), r("XT", k, 320, 16), False, k == 11, k == 11)
+        act(r("XH", 0, 220), r("BX", 0, 220), F.Identity, 0.0, 1.0 / 16384)
+        turn("BZ", "XH", 7, "I16K")
+        tt(sm(D), r("XT", 12, 320, 16), sm(NQ), A.add)
+        ts(r("G4", 0, 220), r("G3", 0, 220), 2047, A.bitwise_and)
+        ts(sm(M), sm(D), CA - 2 * U, A.is_lt, 11 * U, A.mult)
+        tt(sm(E2), r("XT", 13, 320, 16), sm(D), A.add)
+        tt(r("AH", 0, 20), sm(D), sm(M), A.add)
+        tt(sm(BETA), sm(D), sm(M), A.add)
+        tt(sm(T1), sm(E2), sm(N4C), A.max)
+        tt(sm(BQ), sm(BETA), r("AH", 0, 20), A.subtract)
+        tt(r("Y1", 0, 224), ind(r("AH", 0, 20), r("LBC", 0, 14)), r("XH", 0, 224), A.add)
+        act(r("BB", 0, 224), ind(sm(BQ), r("LBC", 0, 14)), F.Identity, -1024.0, 65536.0)
+        mm(r("BZ", 0, 220), r("IH", 0, 128), r("BB", 0, 220), False, False, False)
+        ts(r("Z1", 0, 220), r("Y1", 0, 220), -CA - 0.25, A.add, 0.0, A.max)
+        act(r("Z0", 0, 220), r("Y1", 0, 220), F.Relu, CA + 0.125, -1.0)
+        turn("BZ", "Z1", 7, "N16K")
+        turn("BZ", "Z0", 7, "I16K")
+        turn("BZ", "Z0", 3, "N16K")
+        turn("BZ", "Z1", 0, "I16K")
+        tt(r("UP", 0, 224), ind(sm(E2), r("LBC", 0, 14)), r("KF", 0, 224), A.is_le)
+        tt(r("BASE", 0, 220), r("G4", 0, 220), r("K1", 0, 220), A.min)
+        mm(r("K3", 0, 220), r("NH", 0, 128), r("BB", 0, 220), False, False)
+        mm(r("K3", 0, 220), r("N4K", 0, 128), r("UP", 0, 220), False, False)
+        if not last:
+            act(row("OWN", 12), r("RL%d" % t, 0, 320))
         else:
-            act(r("IMP", 0, 320), land, F.Identity, -OFF)
-        tt(r("G1", 0, 224), ind(r("O0", 0, 224), r("LMG", 0, 14)), r("V0", 0, 224), A.min)
-        tt(r("C", 20, 240), r("G1", 0, 220), r("TOT", 0, 220), A.max)
+            act(r("YI", 0, 320), r("RL%d" % t, 0, 320), F.Identity, OFF)
+            store("a", "d_yi", T.yi[:], r("YI", 0, 320))
+        for z, s, (s1, o1, s2, o2) in (("Z2", 8, (2048.0, A.add, 0.0, A.min)), ("Z3", 9, (-2048.0, A.max, 0.0, A.min)),
+                                       ("Z4", 10, (0.0, A.max, 2048.0, A.min)), ("Z5", 0, (-2048.0, A.add, 0.0, A.max))):
+            ts(r(z, 0, 220), r("BZ", 0, 220), s1, o1, s2, o2)
+            turn("K3", z, s)
+        ts(r("NU", 0, 20), sm(T1), -C0, A.add, 12 * U, A.min)
+        if last:
+            ts(sm(TMP), r("NU", 0, 20), 32.0, A.mult)
+            store("s", "d_yn", T.yn[:], sm(TMP))
+        tt(r("CF" if last else "C", 20, 240), r("K3", 0, 220), r("BASE", 0, 220), A.max)
 
-    store("s", "d_yc", T.yc[:], r("C", 0, 240))
+    store("s", "d_yc", T.yc[:], r("CF", 0, 240))
     for sem in ("d_yi", "d_yn", "d_yc"):
         wait("s", sem, 16)
     for q in ("v", "a", "t", "p"):

@@ -11,16 +11,16 @@ C0 = CA - 1.5 * U
 
 SCRATCH = {}
 for _dt, _bufs in (
-        ("int32", dict(CS=240, NS=32, DS=32, P=224, Q=224, TT=240, CN=240, SI=64, G3=240, G4=240, X=128, X2=128, PC=8,
-                       HJ=16)),
+        ("int32", dict(CS=240, NS=32, DS=32, P=224, Q=224, TT=240, CN=240, SI=64, G3=240, G4=240, PC=8, HJ=16)),
         ("bfloat16", dict(WT=2064, ST=2048, S16=2320, WU=3840, WL=1280, SG=2240, OVER=3840, KB=32, RD=32, CUM=32,
-                          Z=144, ID=128, NI=128, GS=128, BO=128, TR=128, NB=128, KK=240, NEG=32, ONE=128, AH=32)),
-        ("float16", dict(C=256, IMP=320, XT=320, O8=320, IH=128, NH=128, I16K=128, N16K=128, N4K=128, K32=224, ZH=224, XH=224,
-                         BB=224, UP=224, LM=224, Z0=224, Z1=224, Z2=224, Z3=224, Z4=224, Z5=224)),
+                          Z=144, ID=128, NI=128, GS=128, BO=128, TR=128, NB=128, KK=240, NEG=32, ONE=128, X=128, AH=32)),
+        ("float16", dict(C=256, IMP=320, XT=320, O8=320, IH=128, NH=128, I16K=128, N16K=128, N4K=128, K32=224, ZH=224,
+                         KH=224, N4=224, DD=224, AB=224, BB=224, UP=224, LM=224, Z0=224, Z1=224, Z2=224, Z3=224, Z4=224,
+                         Z5=224, Z6=224)),
         ("uint16", dict(WI=224, HI=224, AL=32, INV=32, PL=32, LBC=16, LBU=32)),
         ("float32", dict(CF=256, NU=32, OWN=3840, LA=320, LB=320, C13=240, KS=128, WB=240, M60=64, M61=64, SM=768,
                          B=352, KW=672, Y=352, G1=224, V4=240, BASE=224, YI=320, PF=16, KU=256, KV=224, KF=224,
-                         GSC=224, Y1=224, J4=32, H=64))):
+                         GSC=224, XH=224, Y1=224, IF=128, J4=32, H=64))):
     for _n, _w in _bufs.items():
         SCRATCH[_n] = ("sbuf", [128, _w], _dt)
 PSUM = ("POS", "BX", "BY", "BZ", "K1", "K2", "K3", "TOT")
@@ -169,35 +169,43 @@ def rank_program(g, core, T, topo):
     iota(r("PC", 0, 1), [[0, 1]], 0, 1, False)
     iota(r("H", 0, 16), [[16, 16]], 0)
     iota(r("YI", 0, 320), [[32, 10], [1024, 2], [1, 16]], 0)
-    iota(r("KU", 0, 240), [[4096, 12], [0, 20]], 1)
     fill(r("ONE", 0, 128), 1.0)
     fill(r("IMP", 0, 320), -OFF)
     fill(r("WT", 0, 16), 0.0)
     pick(r("ID", 0, 128), r("ONE", 0, 128), [[-1, 128]], A.is_equal, 0, 1)
+    iota(r("KV", 0, 220), [[1, 11], [0, 20]], -10)
     iota(r("J4", 0, 20), [[1, 20]], 0)
     act(r("K32", 0, 224), r("IMP", 0, 224), F.Identity, 32.0, 0.0)
     act(r("Z", 0, 144), r("IMP", 0, 144), F.Identity, 0.0, 0.0)
     act(r("OVER", 0, 320), r("IMP", 0, 320), F.Identity, 0.0, 0.0)
     act(r("Y", 0, 16), r("IMP", 0, 16), F.Identity, 0.0, 0.0)
     act(r("Y", 336, 352), r("IMP", 0, 16), F.Identity, 0.0, 0.0)
-    act(r("IH", 0, 128), r("ID", 0, 128))
-    act(r("NI", 0, 128), r("ID", 0, 128), F.Identity, 0.0, -1.0)
     act(r("NEG", 0, 32), r("IMP", 0, 32), F.Identity, -7328.0, 0.0)
     act(r("CUM", 0, 32), r("IMP", 0, 32), F.Identity, 0.0, 0.0)
-    act(r("OWN", 3520, 3840), r("IMP", 0, 320))
-    for k in (2, 4, 6, 8, 9, 10, 11, 12):
-        act(r("WU", (k - 1) * 320, k * 320), r("IMP", 0, 320), F.Identity, 0.0, 0.0)
+    act(r("IH", 0, 128), r("ID", 0, 128))
+    act(r("NH", 0, 128), r("ID", 0, 128), F.Identity, 0.0, -1.0)
+    act(r("KH", 0, 220), r("KV", 0, 220))
     pick(r("BO", 0, 128), r("ONE", 0, 128), [[-16, 8], [0, 16]], A.is_ge, 0, 1)
     pick(r("BO", 0, 128), r("BO", 0, 128), [[16, 8], [0, 16]], A.is_ge, 15, -1)
     iota(r("KK", 0, 240), [[-1, 12], [0, 20]], 11)
-    iota(r("X", 0, 128), [[1, 128]], 0, 0, False)
+    pick(r("X", 0, 128), r("ONE", 0, 128), [[0, 8], [-1, 16]], A.is_equal, 0, 1)
     iota(sm(PM), [[0, 10], [16, 2]], 0)
     iota(r("GSC", 0, 220), [[0, 11], [496, 20]], 0)
-    iota(r("KV", 0, 220), [[1, 11], [0, 20]], -10)
     iota(r("KV", 220, 224), [[0, 4]], 0)
     iota(r("WB", 0, 60), [[0, 60]], 0)
     iota(r("B", 0, 16), [[0, 16]], 0)
     iota(r("B", 336, 352), [[0, 16]], 0)
+
+    def room(height):
+        act(r("N4", 0, 224), ind(height, r("LBC", 0, 14)), F.Identity, 0.0, 32.0)
+        mm(r("K2", 0, 220), r("NH", 0, 128), r("KH", 0, 220), True, False, False)
+        mm(r("K2", 0, 220), r("IH", 0, 128), r("N4", 0, 220), False, True)
+
+    def under():
+        act(r("LM", 0, 220), r("K2", 0, 220), F.Relu)
+
+    def cap():
+        act(r("K1", 0, 220), r("LM", 0, 220), F.Identity, -1.0, 4096.0)
 
     ts(r("PC", 1, 2), r("PC", 0, 1), 15, A.bitwise_and)
     ts(r("PC", 2, 3), r("PC", 0, 1), 16, A.bitwise_and)
@@ -214,30 +222,41 @@ def rank_program(g, core, T, topo):
     ts(r("PF", 4, 5), rc, 31.0, A.mult)
     cp(r("LBC", 0, 16), r("H", 32, 48))
     cp(r("AL", 0, 20), r("DS", 0, 20))
-    ts(sm(TMP), r("NS", 0, 20), 4096.0, A.mult)
+    ts(sm(TMP), r("NS", 0, 20), -11.0, A.add, U, A.mult)
+    cp(r("C", 0, 20), r("CS", 0, 20))
+    ts(r("NU", 0, 20), r("NS", 0, 20), U, A.mult)
     emit("v", lambda: g.vector.tensor_copy(ind(r("Y", 16, 336), r("AL", 0, 20))[0], T.YI[:, 0:320]),
          [("YI", 0, 320), ("AL", 0, 20)], [("Y", 16, 336)])
-    tt(r("V4", 0, 240), ind(sm(TMP), r("LBC", 0, 15)), r("KU", 0, 240), A.subtract)
-    ts(r("NU", 0, 20), r("NS", 0, 20), U, A.mult)
-    tt(r("V4", 0, 240), r("V4", 0, 240), r("CS", 0, 240), A.min)
+    room(sm(TMP))
+    act(r("NI", 0, 128), r("ID", 0, 128), F.Identity, 0.0, -1.0)
+    under()
+    cap()
+    act(r("OWN", 3520, 3840), r("IMP", 0, 320))
+    act(r("Z", 15, 143, 16), r("BO", 0, 128, 16), F.Identity, 0.0, 97.0)
+    act(r("KK", 0, 240), r("KK", 0, 240), F.Identity, 0.0, U)
+    act(r("NB", 0, 128), r("BO", 0, 128), F.Identity, 0.0, -BIG)
+    mm(r("TOT", 0, 128), r("X", 0, 128), r("X", 0, 128), True, True)
+    act(r("GS", 0, 128), r("TOT", 0, 128))
+    pick(r("TR", 0, 128), r("NB", 0, 128), [[1, 128]], A.is_gt, 0, -1)
+    pick(r("TR", 0, 128), r("TR", 0, 128), [[1, 128]], A.not_equal, 0, -1, 80 * BIG)
+    for lo, hi in ((2, 2), (4, 4), (6, 6), (8, 12)):
+        iota(r("WU", (lo - 1) * 320, hi * 320), [[0, (hi - lo + 1) * 320]], 0)
     ts(sm(SC), r("J4", 0, 20), 16.0, A.mult, rc, A.add)
-    ts(r("C", 0, 240), r("V4", 0, 240), -1.0, A.max)
+    tr(r("KW", 0, 320), r("Y", 16, 336))
+    ts(r("LBU", 0, 20), r("J4", 0, 20), r("PF", 5, 6), A.add)
+    tt(r("C", 20, 240), r("K1", 0, 220), r("CS", 20, 240), A.min)
+    cp(r("SI", 0, 20), r("KW", 0, 320, 16))
+    cp(sm(T2), r("KW", 0, 320, 16))
 
-    def run_list():
-        tr(r("KW", 0, 320), r("Y", 16, 336))
-        ts(r("LBU", 0, 20), r("J4", 0, 20), r("PF", 5, 6), A.add)
-        cp(r("SI", 0, 20), r("KW", 0, 320, 16))
-        cp(sm(T2), r("KW", 0, 320, 16))
-        chain(8)
+    def run_list(lists):
         ts(r("SI", 20, 40), r("SI", 0, 20), 1024, A.bitwise_and)
         ts(r("SI", 40, 60), r("SI", 0, 20), 1023, A.bitwise_and)
-        ts(r("X2", 0, 128), r("X", 0, 128), 15, A.bitwise_and)
+        lists[0]()
         ts(sm(A1), r("SI", 20, 40), r("PF", 6, 7), A.not_equal, r("PF", 7, 8), A.mult)
         ts(r("SI", 41, 60, 2), r("SI", 41, 60, 2), 16.0, A.add)
-        ts(r("GS", 0, 128), r("X2", 0, 128), rc, A.is_equal)
+        lists[1]()
         tt(sm(A2), sm(A1), r("SI", 40, 60), A.add)
-        strengths(0, 1024, 0)
-        cp(r("PL", 0, 20), sm(A2))
+        lists[2]()
 
     def load_list():
         tr(r("KW", 320, 672), r("Y", 0, 352))
@@ -305,33 +324,38 @@ def rank_program(g, core, T, topo):
     def strengths(lo, hi, frm):
         ts(r("S16", lo, hi), r("ST", frm, frm + hi - lo), 16.0, A.mult, -OFF, A.add)
 
-    def turn(bank, z, s, lhs="IH"):
-        mm(r(bank, 20 * s, 220), r(lhs, 0, 128), r(z, 0, 220 - 20 * s), False, s == 0, s == 0)
-        if s:
-            mm(r(bank, 0, 20 * s), r(lhs, 0, 128), r(z, 220 - 20 * s, 220), False, False, False)
+    HALVES = (("BZ", 0, 120), ("TOT", 120, 220))
+    WHOLE = (("K3", 0, 220),)
+
+    def turn(banks, z, lo, hi, s, lhs, stop=False):
+        for bank, b0, b1 in banks:
+            cuts = [(max(lo + w, b0), min(hi + w, b1), w) for w in (20 * s, 20 * s - 220)]
+            cuts = [c for c in cuts if c[0] < c[1]]
+            for i, (a, b, w) in enumerate(cuts):
+                end = stop and i == len(cuts) - 1
+                mm(r(bank, a - b0, b - b0), r(lhs, 0, 128), r(z, a - w, b - w), False, end, end)
 
     for t in range(RO):
         last = t == RO - 1
         imp = r("IMP", 0, 320) if t == 0 else r("RL%d" % (t - 1), 0, 320)
-        ts(r("WI", 0, 220), r("C", 20, 240), 16.0, A.add)
+        ts(r("WI", 140, 220), r("C", 160, 240), 16.0, A.add)
+        ts(r("WI", 0, 140), r("C", 20, 160), 16.0, A.add)
         mm(r("POS", 0, 220), r("IH", 0, 128), r("K32", 0, 220), True, False, False)
         mm(r("POS", 0, 220), r("IH", 0, 128), r("C", 0, 220), False, True)
         for k in range(7, 0, -1):
             wgath(k)
-        chain(11, imp)
-        tt(r("P", 0, 220), r("C", 20, 240), r("POS", 0, 220), A.mult)
-        chain(10)
-        ts(r("Q", 0, 220), r("P", 0, 220), 5, A.arith_shift_right, 2047 | (1 << 20), A.bitwise_and)
-        chain(9)
-        ts(r("HI", 0, 220), r("Q", 0, 220), 77.0 * t, A.add, 2304.0, A.min)
+        lists = (lambda: tt(r("P", 0, 220), r("C", 20, 240), r("POS", 0, 220), A.mult),
+                 lambda: ts(r("Q", 0, 220), r("P", 0, 220), 5, A.arith_shift_right, 2047 | (1 << 20), A.bitwise_and),
+                 lambda: ts(r("HI", 0, 220), r("Q", 0, 220), 77.0 * t, A.add, 2304.0, A.min))
         if t == 0:
-            run_list()
-            act(r("S16", 1024, 2048), r("ST", 1024, 2048), F.Identity, -OFF, 16.0)
-            act(r("Z", 15, 143, 16), r("BO", 0, 128, 16), F.Identity, 0.0, 97.0)
-            act(r("KK", 0, 240), r("KK", 0, 240), F.Identity, 0.0, U)
-            strengths(2048, 2304, 0)
-        else:
-            chain(8)
+            run_list(lists)
+            lists = (lambda: cp(r("PL", 0, 20), sm(A2)), lambda: strengths(2048, 2304, 0), lambda: strengths(0, 1024, 0))
+        chain(11, imp)
+        for k in (10, 9, 8):
+            lists[10 - k]()
+            chain(k)
+        if t == 0:
+            strengths(1024, 2048, 1024)
         for k in (7, 6, 5, 4):
             weigh(k)
         for j in (7, 6, 4):
@@ -353,42 +377,39 @@ def rank_program(g, core, T, topo):
         comp(8)
         over(7)
         comp(6)
-        gap(3)
         votes("K1", 60, 6)
+        gap(3)
         over(5)
         comp(4)
         mm(r("BX", 0, 320), r("ID", 0, 128), row("SG", 2), True, True)
-        gap(1)
-        over(3)
-        votes("BZ", 0, 3)
         tt(row("OWN", 2), r("K2", 0, 320), row("OWN", 4), A.add)
+        over(3)
+        gap(1)
+        votes("BZ", 0, 3)
         act(r("KS", 60, 120), r("K1", 120, 180))
         act(r("C13", 0, 240), r("C", 0, 240), F.Identity, float(t), 13.0)
         tt(r("OVER", 640, 960), r("BX", 0, 320), row("OWN", 2), A.is_lt)
         over(1)
         votes("BY", 0, 0)
-        if t == 0:
-            act(r("NB", 0, 128), r("BO", 0, 128), F.Identity, 0.0, -BIG)
-            pick(r("TR", 0, 128), r("NB", 0, 128), [[1, 128]], A.is_gt, 0, -1)
-            pick(r("TR", 0, 128), r("TR", 0, 128), [[1, 128]], A.not_equal, 0, -1, 80 * BIG)
         tt(r("M60", 0, 60), r("K1", 60, 120), r("KS", 60, 120), A.max)
         tt(r("TT", 120, 240), r("K1", 60, 180), r("C13", 120, 240), A.add)
         tt(r("TT", 60, 120), r("BZ", 0, 60), r("C13", 60, 120), A.add)
         tt(r("M61", 0, 60), r("BZ", 0, 60), r("M60", 0, 60), A.max)
+        ts(sm(NA), r("NU", 0, 20), -10 * U, A.add, U, A.min)
         ts(r("CN", 60, 240), r("TT", 60, 240), 2047, A.bitwise_and)
         tt(r("M61", 20, 40), r("M61", 0, 20), r("M61", 20, 40), A.max)
+        mm(r("TOT", 0, 20), r("ID", 0, 128), r("NEG", 0, 20), True, False, False)
+        tt(r("TT", 0, 60), r("BY", 0, 60), r("C13", 0, 60), A.add)
+        tt(r("M60", 0, 40), r("BY", 20, 60), r("M61", 20, 60), A.max)
         cp(r("WB", 60, 240), r("CN", 60, 240))
         act(row("OWN", 7), r("O8", 0, 320))
         act(r("B", 16, 336), ind(r("WB", 0, 240), r("LBU", 0, 20)))
         built = ("a", count["a"])
-        mm(r("TOT", 0, 20), r("ID", 0, 128), r("NEG", 0, 20), True, False, False)
-        tt(r("M60", 0, 40), r("BY", 20, 60), r("M61", 20, 60), A.max)
-        tt(r("TT", 0, 60), r("BY", 0, 60), r("C13", 0, 60), A.add)
         tt(r("KB", 0, 20), r("M60", 0, 20), r("M60", 20, 40), A.max)
         mm(r("TOT", 0, 20), r("GS", 0, 128), r("KB", 0, 20), False, True)
         tt(sm(KEY), r("M60", 0, 20), r("M60", 20, 40), A.max)
         ts(r("CN", 0, 60), r("TT", 0, 60), 2047, A.bitwise_and)
-        ts(sm(THR), sm(KEY), 872.5, A.is_lt, 1.0e6, A.mult)
+        ts(sm(THR), r("KB", 0, 20), 824.0, A.is_lt, 1.0e6, A.mult)
         cp(r("SI", 0, 20), sm(KEY))
         tt(r("RD", 0, 20), r("TOT", 0, 20), sm(THR), A.is_gt)
         tt(sm(FR), sm(KEY), r("SI", 0, 20), A.subtract)
@@ -400,62 +421,57 @@ def rank_program(g, core, T, topo):
         act(row("OWN", 1), row("OWN", 2))
         cp(r("B", 17, 336, 16), r("CN", 20, 40), built)
         cp(r("B", 18, 336, 16), r("CN", 40, 60), built)
+        ts(sm(A1), sm(FR), U, A.add, -10240.0, A.mult)
+        tt(sm(DK), sm(FR), sm(NA), A.add)
         tt(r("B", 29, 336, 16), r("POS", 0, 20), r("NU", 0, 20), A.min, built)
+        ts(sm(SL), r("POS", 0, 20), 0.0, A.is_gt)
+        cp(r("WB", 0, 60), r("CN", 0, 60))
         tr(r("KW", 0, 320), r("B", 16, 336))
         tr(r("KW", 320, 672), r("B", 0, 352))
         act(row("OWN", 3), row("OWN", 4))
+        act(row("OWN", 5), row("OWN", 6))
+        tt(sm(A1), sm(A1), sm(SL), A.mult)
+        tt(sm(DK), sm(DK), sm(SL), A.mult)
         act(r("MK%d" % t, 0, 160), ind(r("KW", 0, 672), r("PL", 0, 10)), F.Relu)
         ts(r("MK%d" % t, 160, 320), ind(r("KW", 0, 672), r("PL", 10, 20)), 0.0, A.max)
         send(t, "MK%d" % t, "RK%d" % t, "rk%d" % t)
         if t == 0:
             load_list()
-        act(row("OWN", 5), row("OWN", 6))
         act(row("OWN", 8), r("O8", 0, 320))
-        ts(sm(SL), r("POS", 0, 20), 0.0, A.is_gt)
-        ts(sm(A1), sm(FR), U, A.add, -10240.0, A.mult)
-        ts(sm(NA), r("NU", 0, 20), -10 * U, A.add, U, A.min)
-        tt(sm(A1), sm(A1), sm(SL), A.mult)
-        tt(sm(DK), sm(FR), sm(NA), A.add)
         tt(sm(A2), sm(A1), sm(SC2), A.add)
-        tt(sm(DK), sm(DK), sm(SL), A.mult)
-        cp(r("AL", 0, 20), sm(A2))
         tt(sm(NQ0), sm(NA), sm(DK), A.subtract)
-        act(r("BY", 0, 220), r("GSC", 0, 220), F.Identity, float(997 * t - ((t - 13) & 2047)))
-        act(r("TOT", 0, 220), r("C", 20, 240), F.Relu, 0.0, -1.0)
+        act(r("DD", 0, 220), r("C", 20, 240), F.Relu, 0.0, -4.0)
+        cp(r("AL", 0, 20), sm(A2))
+        ts(sm(NQ), sm(NQ0), C0, A.add)
+        ts(sm(N4C), sm(NQ0), C0 + 11 * U, A.add)
+        act(r("G1", 0, 220), r("GSC", 0, 220), F.Identity, 997.0 * t - 32768)
         if t == 0:
             act(r("KF", 0, 224), r("KV", 0, 224), F.Identity, 11 * U + C0, U)
-            act(r("KV", 0, 224), r("KV", 0, 224), F.Identity, 0.0, U)
             act(r("ZH", 0, 224), r("K32", 0, 224), F.Identity, 0.0, 0.0)
-            act(r("NH", 0, 128), r("ID", 0, 128), F.Identity, 0.0, -1.0)
-            act(r("I16K", 0, 128), r("ID", 0, 128), F.Identity, 0.0, 16384.0)
-            act(r("N16K", 0, 128), r("ID", 0, 128), F.Identity, 0.0, -16384.0)
-            act(r("N4K", 0, 128), r("ID", 0, 128), F.Identity, 0.0, -4096.0)
             act(r("XH", 220, 224), r("K32", 0, 4), F.Identity, 0.0, 0.0)
+            for name, x in (("IF", 1), ("I16K", 16384), ("N16K", -16384), ("N4K", -4096)):
+                act(r(name, 0, 128), r("ID", 0, 128), F.Identity, 0.0, x)
+        mm(r("BY", 0, 220), r("IF", 0, 128), r("WB", 0, 220), True, False, False)
+        mm(r("BY", 0, 220), r("I16K", 0, 128), r("DD", 0, 220), False, False, False)
+        mm(r("BY", 0, 220), r("IF", 0, 128), r("G1", 0, 220), False, True)
+        room(sm(NQ0))
+        under()
         tt(r("LA", 0, 320), ind(r("OWN", 0, 3840), r("AL", 0, 20)), imp, A.subtract)
-        ts(sm(NQ), sm(NQ0), C0, A.add)
+        cp(r("CF" if last else "C", 0, 20), r("CN", 0, 20))
         tt(r("LB", 0, 320), ind(r("WU", 0, 3840), r("AL", 0, 20)), r("LA", 0, 320), A.add)
         act(r("ML%d" % t, 0, 320), ind(r("LB", 0, 320), r("INV", 0, 20)), F.Identity, -OFF)
         send(t, "ML%d" % t, "RL%d" % t, "rl%d" % t)
-        tt(r("V4", 0, 224), ind(sm(NQ0), r("LBC", 0, 14)), r("KV", 0, 224), A.subtract)
-        tt(r("G1", 0, 220), r("CN", 0, 220), r("BY", 0, 220), A.add)
-        act(r("LM", 0, 220), r("V4", 0, 220), F.Relu, 0.0, 32.0)
-        act(r("K1", 0, 220), r("LM", 0, 220), F.Identity, -1.0, 4096.0)
-        cp(r("CF" if last else "C", 0, 20), r("CN", 0, 20))
-        tt(r("K2", 0, 220), r("G1", 0, 220), r("TOT", 0, 220), A.mult)
-        ts(sm(N4C), sm(NQ0), C0 + 11 * U, A.add)
-        tt(r("G3", 0, 220), r("K2", 0, 220), r("CN", 20, 240), A.add)
+        tt(r("G3", 0, 220), r("BY", 0, 220), r("CN", 20, 240), A.max)
+        ts(r("G4", 0, 220), r("G3", 0, 220), 2047, A.bitwise_and)
         mm(r("BX", 0, 220), r("IH", 0, 128), r("ZH", 0, 220), True, False, False)
-        mm(r("BZ", 0, 220), r("IH", 0, 128), r("ZH", 0, 220), True, False, False)
-        mm(r("K3", 0, 220), r("N4K", 0, 128), r("LM", 0, 220), True, False)
         arrival(t, "RK%d" % t, "rk%d" % t)
         arrival(t, "RL%d" % t, "rl%d" % t)
         tr(r("XT", 0, 320), r("RK%d" % t, 0, 320))
         for k in range(1, 12):
             mm(r("BX", 20 * k - 20, 20 * k), r("IH", 0, 128), r("XT", k, 320, 16), False, k == 11, k == 11)
-        act(r("XH", 0, 220), r("BX", 0, 220), F.Identity, 0.0, 1.0 / 16384)
-        turn("BZ", "XH", 7, "I16K")
+        mm(r("K3", 0, 220), r("N4K", 0, 128), r("LM", 0, 220), True, False)
+        act(r("XH", 0, 220), r("BX", 0, 220), F.Identity, -CA - 0.125, 1.0 / 16384)
         tt(sm(D), r("XT", 12, 320, 16), sm(NQ), A.add)
-        ts(r("G4", 0, 220), r("G3", 0, 220), 2047, A.bitwise_and)
         ts(sm(M), sm(D), CA - 2 * U, A.is_lt, 11 * U, A.mult)
         tt(sm(E2), r("XT", 13, 320, 16), sm(D), A.add)
         tt(r("AH", 0, 20), sm(D), sm(M), A.add)
@@ -463,32 +479,44 @@ def rank_program(g, core, T, topo):
         tt(sm(T1), sm(E2), sm(N4C), A.max)
         tt(sm(BQ), sm(BETA), r("AH", 0, 20), A.subtract)
         tt(r("Y1", 0, 224), ind(r("AH", 0, 20), r("LBC", 0, 14)), r("XH", 0, 224), A.add)
+        act(r("AB", 0, 224), ind(r("AH", 0, 20), r("LBC", 0, 14)), F.Identity, 16384 * (CA + 0.125), -16384.0)
         act(r("BB", 0, 224), ind(sm(BQ), r("LBC", 0, 14)), F.Identity, -1024.0, 65536.0)
-        mm(r("BZ", 0, 220), r("IH", 0, 128), r("BB", 0, 220), False, False, False)
-        ts(r("Z1", 0, 220), r("Y1", 0, 220), -CA - 0.25, A.add, 0.0, A.max)
-        act(r("Z0", 0, 220), r("Y1", 0, 220), F.Relu, CA + 0.125, -1.0)
-        turn("BZ", "Z1", 7, "N16K")
-        turn("BZ", "Z0", 7, "I16K")
-        turn("BZ", "Z0", 3, "N16K")
-        turn("BZ", "Z1", 0, "I16K")
+        for bank, lo, hi in HALVES:
+            mm(r(bank, 0, hi - lo), r("IH", 0, 128), r("AB", lo, hi), True, False, False)
+        ts(r("Z1", 0, 220), r("Y1", 0, 220), 0.0, A.max, 0.125, A.min)
+        ts(r("Z2", 0, 220), r("Y1", 0, 220), -0.125, A.add, 0.0, A.max)
+        act(r("Z0", 0, 220), r("Y1", 0, 220), F.Relu, 0.0, -1.0)
+        cap()
+        for bank, lo, hi in HALVES:
+            mm(r(bank, 0, hi - lo), r("IH", 0, 128), r("BB", lo, hi), False, False, False)
+        turn(HALVES, "Z1", 0, 220, 7, "I16K")
+        turn(HALVES, "Z0", 0, 220, 3, "N16K")
+        turn(HALVES, "Z2", 0, 220, 0, "I16K", True)
         tt(r("UP", 0, 224), ind(sm(E2), r("LBC", 0, 14)), r("KF", 0, 224), A.is_le)
-        tt(r("BASE", 0, 220), r("G4", 0, 220), r("K1", 0, 220), A.min)
         mm(r("K3", 0, 220), r("NH", 0, 128), r("BB", 0, 220), False, False)
         mm(r("K3", 0, 220), r("N4K", 0, 128), r("UP", 0, 220), False, False)
+        for h in (0, 1):
+            bank, lo, hi = HALVES[h]
+            ts(r("Z3", lo, hi), r(bank, 0, hi - lo), -2048.0, A.max, 0.0, A.min)
+            ts(r("Z4", lo, hi), r(bank, 0, hi - lo), 0.0, A.max, 2048.0, A.min)
+            bank, lo2, hi2 = HALVES[1 - h]
+            act(r("Z5", lo2, hi2), r(bank, 0, hi2 - lo2), F.Relu, -2048.0, -1.0)
+            act(r("Z6", lo2, hi2), r(bank, 0, hi2 - lo2), F.Relu, -2048.0, 1.0)
+            turn(WHOLE, "Z3", lo, hi, 9, "IH")
+            turn(WHOLE, "Z5", lo2, hi2, 8, "NH")
+            turn(WHOLE, "Z4", lo, hi, 10, "IH")
+            turn(WHOLE, "Z6", lo2, hi2, 0, "IH", h == 1)
+        tt(r("BASE", 0, 220), r("G4", 0, 220), r("K1", 0, 220), A.min)
+        ts(r("NU", 0, 20), sm(T1), -C0, A.add, 12 * U, A.min)
         if not last:
             act(row("OWN", 12), r("RL%d" % t, 0, 320))
         else:
             act(r("YI", 0, 320), r("RL%d" % t, 0, 320), F.Identity, OFF)
             store("a", "d_yi", T.yi[:], r("YI", 0, 320))
-        for z, s, (s1, o1, s2, o2) in (("Z2", 8, (2048.0, A.add, 0.0, A.min)), ("Z3", 9, (-2048.0, A.max, 0.0, A.min)),
-                                       ("Z4", 10, (0.0, A.max, 2048.0, A.min)), ("Z5", 0, (-2048.0, A.add, 0.0, A.max))):
-            ts(r(z, 0, 220), r("BZ", 0, 220), s1, o1, s2, o2)
-            turn("K3", z, s)
-        ts(r("NU", 0, 20), sm(T1), -C0, A.add, 12 * U, A.min)
-        if last:
             ts(sm(TMP), r("NU", 0, 20), 32.0, A.mult)
             store("s", "d_yn", T.yn[:], sm(TMP))
-        tt(r("CF" if last else "C", 20, 240), r("K3", 0, 220), r("BASE", 0, 220), A.max)
+        for lo, hi in (((0, 220),) if last else ((140, 220), (0, 140))):
+            tt(r("CF" if last else "C", 20 + lo, 20 + hi), r("K3", lo, hi), r("BASE", lo, hi), A.max)
 
     store("s", "d_yc", T.yc[:], r("CF", 0, 240))
     for sem in ("d_yi", "d_yn", "d_yc"):

@@ -11,16 +11,16 @@ C0 = CA - 1.5 * U
 
 SCRATCH = {}
 for _dt, _bufs in (
-        ("int32", dict(CS=240, NS=32, DS=32, P=224, Q=224, TT=240, CN=240, SI=64, G3=240, G4=240, PC=8, HJ=16)),
-        ("bfloat16", dict(WT=2064, ST=2048, S16=2320, WU=3840, WL=1280, SG=2240, OVER=3840, KB=32, RD=32, CUM=32,
-                          Z=144, ID=128, NI=128, GS=128, BO=128, TR=128, NB=128, KK=240, NEG=32, ONE=128, X=128, AH=32)),
-        ("float16", dict(C=256, IMP=320, XT=320, O8=320, IH=128, NH=128, I16K=128, N16K=128, N4K=128, K32=224, ZH=224,
-                         KH=224, N4=224, DD=224, AB=224, BB=224, UP=224, LM=224, Z0=224, Z1=224, Z2=224, Z3=224, Z4=224,
-                         Z5=224, Z6=224)),
-        ("uint16", dict(WI=224, HI=224, AL=32, INV=32, PL=32, LBC=16, LBU=32)),
-        ("float32", dict(CF=256, NU=32, OWN=3840, LA=320, LB=320, C13=240, KS=128, WB=240, M60=64, M61=64, SM=768,
-                         B=352, KW=672, Y=352, G1=224, V4=240, BASE=224, YI=320, PF=16, KU=256, KV=224, KF=224,
-                         GSC=224, XH=224, Y1=224, IF=128, J4=32, H=64))):
+        ("int32", dict(CS=240, NS=32, DS=32, P=224, Q=224, TT=240, CN=240, SI=32, SJ=64, G3=240, G4=240, PC=8, HJ=16)),
+        ("bfloat16", dict(WT=2064, ST=2048, S16=2320, WU=3840, SG=2240, OVER=3840, KB=32, RD=32, CUM=32,
+                          Z=144, ID=128, NI=128, GS=128, BO=128, TR=128, NB=128, KK=240, NEG=32, ONE=128, X=128, AH=32, KH=224)),
+        ("float16", dict(C=256, IMP=320, XT=320, O8=320, IH=128, NH=128, I16K=128, N16K=128, N4K=128, K32=224, ZH=352,
+                         N4=224, DD=224, AB=224, BB=224, UP=224, LM=224, Z0=224, Z1=224, Z2=224, Z3=224, Z4=224,
+                         Z5=224, Z6=224, NU=32, FR=32, CH=240, G1=224)),
+        ("uint16", dict(WI=224, HI=224, AL=32, INV=32, PL=32, LBC=16)),
+        ("float32", dict(CF=256, OWN=3840, LA=320, LB=320, C13=240, KS=128, M60=64, M61=64, SM=768,
+                         KW=672, Y=352, BASE=224, YI=320, PF=16, KF=224,
+                         XH=224, Y1=224, J4=32, H=64))):
     for _n, _w in _bufs.items():
         SCRATCH[_n] = ("sbuf", [128, _w], _dt)
 PSUM = ("POS", "BX", "BY", "BZ", "K1", "K2", "K3", "TOT")
@@ -157,48 +157,47 @@ def rank_program(g, core, T, topo):
         frm = T.cores[(rank - 1 - t % (n_ranks - 1)) % n_ranks]
         log[name] = [(0, 320, True, sem, len(topo.engines(frm, core)))]
 
-    (KEY, THR, FR, SL, A1, A2, NA, DK, NQ0, NQ, N4C, D, M, BETA, BQ, E2, SC, SC2, TMP, PM, T1, T2) = range(22)
+    (KEY, THR, FR, SL, A1, A2, NA, DK, NQ0, NQ, N4C, D, M, BETA, BQ, E2, SC, SC2, TMP, PM, T1, T2, GM) = range(23)
 
-    load("s", "d_cs", r("CS", 0, 240), T.cs[:])
     load("s", "d_ns", r("NS", 0, 20), T.ns[:])
-    load("s", "d_ds", r("DS", 0, 20), T.ds[:])
+    load("a", "d_ds", r("DS", 0, 20), T.ds[:])
+    load("s", "d_cs", r("CS", 0, 240), T.cs[:])
     load("s", "d_wt", r("WT", 16, 2064), T.wt[:])
     load("s", "d_s0", r("ST", 0, 1024), T.st[:, 0:1024])
     load("s", "d_s1", r("ST", 1024, 2048), T.st[:, 1024:2048])
 
     iota(r("PC", 0, 1), [[0, 1]], 0, 1, False)
     iota(r("H", 0, 16), [[16, 16]], 0)
-    iota(r("YI", 0, 320), [[32, 10], [1024, 2], [1, 16]], 0)
     fill(r("ONE", 0, 128), 1.0)
     fill(r("IMP", 0, 320), -OFF)
     fill(r("WT", 0, 16), 0.0)
     pick(r("ID", 0, 128), r("ONE", 0, 128), [[-1, 128]], A.is_equal, 0, 1)
-    iota(r("KV", 0, 220), [[1, 11], [0, 20]], -10)
+    iota(r("YI", 0, 320), [[32, 10], [1024, 2], [1, 16]], 0)
+    iota(r("KH", 0, 220), [[-1, 11], [0, 20]], 10)
     iota(r("J4", 0, 20), [[1, 20]], 0)
     act(r("K32", 0, 224), r("IMP", 0, 224), F.Identity, 32.0, 0.0)
+    act(r("ZH", 0, 176), r("IMP", 0, 176), F.Identity, 0.0, 0.0)
+    act(r("ZH", 176, 352), r("IMP", 0, 176), F.Identity, 0.0, 0.0)
+    act(r("IH", 0, 128), r("ID", 0, 128))
+    act(r("NI", 0, 128), r("ID", 0, 128), F.Identity, 0.0, -1.0)
     act(r("Z", 0, 144), r("IMP", 0, 144), F.Identity, 0.0, 0.0)
     act(r("OVER", 0, 320), r("IMP", 0, 320), F.Identity, 0.0, 0.0)
     act(r("Y", 0, 16), r("IMP", 0, 16), F.Identity, 0.0, 0.0)
     act(r("Y", 336, 352), r("IMP", 0, 16), F.Identity, 0.0, 0.0)
+    act(r("KH", 220, 224), r("IMP", 0, 4), F.Identity, 0.0, 0.0)
     act(r("NEG", 0, 32), r("IMP", 0, 32), F.Identity, -7328.0, 0.0)
     act(r("CUM", 0, 32), r("IMP", 0, 32), F.Identity, 0.0, 0.0)
-    act(r("IH", 0, 128), r("ID", 0, 128))
     act(r("NH", 0, 128), r("ID", 0, 128), F.Identity, 0.0, -1.0)
-    act(r("KH", 0, 220), r("KV", 0, 220))
+    act(r("OWN", 3520, 3840), r("IMP", 0, 320))
+    pick(r("X", 0, 128), r("ONE", 0, 128), [[0, 8], [-1, 16]], A.is_equal, 0, 1)
     pick(r("BO", 0, 128), r("ONE", 0, 128), [[-16, 8], [0, 16]], A.is_ge, 0, 1)
     pick(r("BO", 0, 128), r("BO", 0, 128), [[16, 8], [0, 16]], A.is_ge, 15, -1)
     iota(r("KK", 0, 240), [[-1, 12], [0, 20]], 11)
-    pick(r("X", 0, 128), r("ONE", 0, 128), [[0, 8], [-1, 16]], A.is_equal, 0, 1)
     iota(sm(PM), [[0, 10], [16, 2]], 0)
-    iota(r("GSC", 0, 220), [[0, 11], [496, 20]], 0)
-    iota(r("KV", 220, 224), [[0, 4]], 0)
-    iota(r("WB", 0, 60), [[0, 60]], 0)
-    iota(r("B", 0, 16), [[0, 16]], 0)
-    iota(r("B", 336, 352), [[0, 16]], 0)
 
     def room(height):
         act(r("N4", 0, 224), ind(height, r("LBC", 0, 14)), F.Identity, 0.0, 32.0)
-        mm(r("K2", 0, 220), r("NH", 0, 128), r("KH", 0, 220), True, False, False)
+        mm(r("K2", 0, 220), r("ID", 0, 128), r("KH", 0, 220), True, False, False)
         mm(r("K2", 0, 220), r("IH", 0, 128), r("N4", 0, 220), False, True)
 
     def under():
@@ -213,59 +212,59 @@ def rank_program(g, core, T, topo):
     cp(r("PF", 0, 3), r("PC", 0, 3))
     rc = r("PF", 1, 2)
     ts(r("H", 0, 16), r("H", 0, 16), rc, A.add)
-    ts(r("PF", 5, 6), rc, 11.0, A.min, 20.0, A.mult)
-    ts(r("HJ", 0, 16), r("H", 0, 16), -9.5, A.add, 0.05, A.mult)
     ts(r("PF", 6, 7), r("PF", 2, 3), 64.0, A.mult)
-    ts(r("H", 16, 32), r("HJ", 0, 16), -20.0, A.mult)
     ts(r("PF", 7, 8), r("PF", 2, 3), -2.0, A.mult, 352.0, A.add)
-    tt(r("H", 32, 48), r("H", 16, 32), r("H", 0, 16), A.add)
-    ts(r("PF", 4, 5), rc, 31.0, A.mult)
-    cp(r("LBC", 0, 16), r("H", 32, 48))
+    ts(r("HJ", 0, 16), r("H", 0, 16), -9.5, A.add, 0.05, A.mult)
     cp(r("AL", 0, 20), r("DS", 0, 20))
-    ts(sm(TMP), r("NS", 0, 20), -11.0, A.add, U, A.mult)
-    cp(r("C", 0, 20), r("CS", 0, 20))
+    ts(r("KB", 0, 20), r("NS", 0, 20), -11.5, A.add)
     ts(r("NU", 0, 20), r("NS", 0, 20), U, A.mult)
     emit("v", lambda: g.vector.tensor_copy(ind(r("Y", 16, 336), r("AL", 0, 20))[0], T.YI[:, 0:320]),
          [("YI", 0, 320), ("AL", 0, 20)], [("Y", 16, 336)])
-    room(sm(TMP))
-    act(r("NI", 0, 128), r("ID", 0, 128), F.Identity, 0.0, -1.0)
-    under()
-    cap()
-    act(r("OWN", 3520, 3840), r("IMP", 0, 320))
-    act(r("Z", 15, 143, 16), r("BO", 0, 128, 16), F.Identity, 0.0, 97.0)
-    act(r("KK", 0, 240), r("KK", 0, 240), F.Identity, 0.0, U)
-    act(r("NB", 0, 128), r("BO", 0, 128), F.Identity, 0.0, -BIG)
-    mm(r("TOT", 0, 128), r("X", 0, 128), r("X", 0, 128), True, True)
-    act(r("GS", 0, 128), r("TOT", 0, 128))
-    pick(r("TR", 0, 128), r("NB", 0, 128), [[1, 128]], A.is_gt, 0, -1)
-    pick(r("TR", 0, 128), r("TR", 0, 128), [[1, 128]], A.not_equal, 0, -1, 80 * BIG)
-    for lo, hi in ((2, 2), (4, 4), (6, 6), (8, 12)):
-        iota(r("WU", (lo - 1) * 320, hi * 320), [[0, (hi - lo + 1) * 320]], 0)
+    mm(r("K2", 0, 352), r("IH", 0, 128), r("ZH", 0, 352), True, True)
+    for at in range(0, 220, 20):
+        mm(r("K1", at, at + 20), r("ID", 0, 128), r("KB", 0, 20), at == 0, False, False)
+    mm(r("K1", 0, 220), r("ID", 0, 128), r("KH", 0, 220), False, True)
+    ts(r("K3", 0, 220), r("K1", 0, 220), -1.0 / 4096, A.max, 4096.0, A.mult)
+    cp(r("C", 0, 20), r("CS", 0, 20))
     ts(sm(SC), r("J4", 0, 20), 16.0, A.mult, rc, A.add)
-    tr(r("KW", 0, 320), r("Y", 16, 336))
-    ts(r("LBU", 0, 20), r("J4", 0, 20), r("PF", 5, 6), A.add)
-    tt(r("C", 20, 240), r("K1", 0, 220), r("CS", 20, 240), A.min)
-    cp(r("SI", 0, 20), r("KW", 0, 320, 16))
-    cp(sm(T2), r("KW", 0, 320, 16))
+    tt(r("C", 20, 240), r("K3", 0, 220), r("CS", 20, 240), A.min)
 
-    def run_list(lists):
-        ts(r("SI", 20, 40), r("SI", 0, 20), 1024, A.bitwise_and)
-        ts(r("SI", 40, 60), r("SI", 0, 20), 1023, A.bitwise_and)
-        lists[0]()
-        ts(sm(A1), r("SI", 20, 40), r("PF", 6, 7), A.not_equal, r("PF", 7, 8), A.mult)
-        ts(r("SI", 41, 60, 2), r("SI", 41, 60, 2), 16.0, A.add)
-        lists[1]()
-        tt(sm(A2), sm(A1), r("SI", 40, 60), A.add)
-        lists[2]()
+    def matrices():
+        mm(r("TOT", 0, 128), r("X", 0, 128), r("X", 0, 128), True, True)
+        act(r("GS", 0, 128), r("TOT", 0, 128))
+        act(r("Z", 15, 143, 16), r("BO", 0, 128, 16), F.Identity, 0.0, 97.0)
+        act(r("NB", 0, 128), r("BO", 0, 128), F.Identity, 0.0, -1.0)
+        pick(r("TR", 0, 128), r("NB", 0, 128), [[1, 128]], A.is_gt, 0, -1)
+        pick(r("TR", 0, 128), r("TR", 0, 128), [[1, 128]], A.not_equal, 0, -1, 80.0)
+        iota(r("WU", 7 * 320, 12 * 320), [[0, 5 * 320]], 0)
+
+    spare = [lambda: tr(r("KW", 0, 320), r("Y", 16, 336)),
+             lambda: cp(r("SJ", 0, 20), r("KW", 0, 320, 16)),
+             lambda: cp(sm(T2), r("KW", 0, 320, 16)),
+             lambda: ts(r("SJ", 20, 40), r("SJ", 0, 20), 1024, A.bitwise_and),
+             lambda: ts(r("SJ", 40, 60), r("SJ", 0, 20), 1023, A.bitwise_and),
+             lambda: ts(sm(T1), r("SJ", 20, 40), r("PF", 6, 7), A.not_equal, r("PF", 7, 8), A.mult),
+             lambda: ts(r("SJ", 41, 60, 2), r("SJ", 41, 60, 2), 16.0, A.add),
+             lambda: tt(sm(T1), sm(T1), r("SJ", 40, 60), A.add),
+             lambda: cp(r("PL", 0, 20), sm(T1))]
+
+    def idle(n=1):
+        for _ in range(min(n, len(spare))):
+            spare.pop(0)()
 
     def load_list():
         tr(r("KW", 320, 672), r("Y", 0, 352))
         ts(sm(PM), sm(PM), r("PF", 2, 3), A.not_equal)
+        ts(r("H", 16, 32), r("HJ", 0, 16), -20.0, A.mult)
         tt(sm(T1), r("KW", 336, 656, 16), sm(T2), A.subtract)
-        ts(r("GSC", 0, 220), r("GSC", 0, 220), r("PF", 4, 5), A.add)
+        ts(r("SJ", 0, 20), sm(SC), 31.0, A.mult)
+        tt(r("H", 32, 48), r("H", 16, 32), r("H", 0, 16), A.add)
         tt(sm(T1), sm(T1), sm(PM), A.mult)
-        ts(sm(SC2), sm(SC), 3520.0, A.add)
+        ts(r("SJ", 20, 40), r("SJ", 0, 20), 2047, A.bitwise_and)
+        cp(r("LBC", 0, 16), r("H", 32, 48))
         tt(sm(T1), sm(T1), sm(T2), A.add)
+        cp(sm(GM), r("SJ", 20, 40))
+        ts(sm(SC2), sm(SC), 3520.0, A.add)
         ts(sm(T2), sm(T1), 1023.5, A.is_gt, -1008.0, A.mult)
         tt(sm(T1), sm(T1), sm(T2), A.add)
         cp(r("INV", 0, 20), sm(T1))
@@ -274,10 +273,10 @@ def rank_program(g, core, T, topo):
         return r(name, (k - 1) * 320, k * 320)
 
     def wrow(k):
-        return row("WU", k) if k % 2 else row("WL", k // 2)
+        return row("WU", k)
 
-    def wgath(k):
-        act(wrow(k), ind(r("WT", 0, 2064), r("WI", 20 * (k - 1), 20 * k)))
+    def wgath(lo, hi):
+        act(r("WU", (lo - 1) * 320, hi * 320), ind(r("WT", 0, 2064), r("WI", 20 * (lo - 1), 20 * hi)))
 
     def sgath(lo, hi):
         act(r("SG", (lo - 1) * 320, hi * 320), ind(r("S16", 0, 2320), r("HI", 20 * (lo - 1), 20 * hi)))
@@ -312,8 +311,10 @@ def rank_program(g, core, T, topo):
         else:
             tt(r("OVER", k * 320, k * 320 + 320), row("SG", k), r(SUMS[k], 0, 320), A.is_lt)
 
-    def comp(k):
-        tt(r("OVER", k * 320, k * 320 + 320), ind(r("S16", 0, 2320), r("HI", 20 * (k - 1), 20 * k)), own(k), A.is_lt)
+    def comp(k, hi=None):
+        loads = r("OWN", (k - 1) * 320, hi * 320) if hi else own(k)
+        hi = hi or k
+        tt(r("OVER", k * 320, hi * 320 + 320), ind(r("S16", 0, 2320), r("HI", 20 * (k - 1), 20 * hi)), loads, A.is_lt)
 
     def votes(bank, at, k0):
         kp = r(bank, at, at + 60)
@@ -323,6 +324,9 @@ def rank_program(g, core, T, topo):
 
     def strengths(lo, hi, frm):
         ts(r("S16", lo, hi), r("ST", frm, frm + hi - lo), 16.0, A.mult, -OFF, A.add)
+
+    def field(f, lhs, x, stop=False):
+        mm(r("K2", 16 + f, 336, 16), r(lhs, 0, 128), x, f == 13, stop, stop)
 
     HALVES = (("BZ", 0, 120), ("TOT", 120, 220))
     WHOLE = (("K3", 0, 220),)
@@ -338,33 +342,41 @@ def rank_program(g, core, T, topo):
     for t in range(RO):
         last = t == RO - 1
         imp = r("IMP", 0, 320) if t == 0 else r("RL%d" % (t - 1), 0, 320)
-        ts(r("WI", 140, 220), r("C", 160, 240), 16.0, A.add)
-        ts(r("WI", 0, 140), r("C", 20, 160), 16.0, A.add)
+        ts(r("WI", 120, 220), r("C", 140, 240), 16.0, A.add)
+        ts(r("WI", 0, 120), r("C", 20, 140), 16.0, A.add)
         mm(r("POS", 0, 220), r("IH", 0, 128), r("K32", 0, 220), True, False, False)
         mm(r("POS", 0, 220), r("IH", 0, 128), r("C", 0, 220), False, True)
-        for k in range(7, 0, -1):
-            wgath(k)
+        for lo, hi in ((7, 7), (5, 6), (3, 4), (1, 2)):
+            if t == 0 and lo == 7:
+                matrices()
+            if t == 0 and lo == 5:
+                act(r("KK", 0, 240), r("KK", 0, 240), F.Identity, 0.0, U)
+            if t == 0 and lo == 1:
+                act(r("S16", 1536, 2048), r("ST", 1536, 2048), F.Identity, -OFF, 16.0)
+            wgath(lo, hi)
         lists = (lambda: tt(r("P", 0, 220), r("C", 20, 240), r("POS", 0, 220), A.mult),
                  lambda: ts(r("Q", 0, 220), r("P", 0, 220), 5, A.arith_shift_right, 2047 | (1 << 20), A.bitwise_and),
                  lambda: ts(r("HI", 0, 220), r("Q", 0, 220), 77.0 * t, A.add, 2304.0, A.min))
         if t == 0:
-            run_list(lists)
-            lists = (lambda: cp(r("PL", 0, 20), sm(A2)), lambda: strengths(2048, 2304, 0), lambda: strengths(0, 1024, 0))
+            for make in lists[:2]:
+                idle()
+                make()
+            lists = (lists[2], lambda: idle(3), lambda: strengths(0, 1024, 0))
         chain(11, imp)
         for k in (10, 9, 8):
             lists[10 - k]()
             chain(k)
         if t == 0:
-            strengths(1024, 2048, 1024)
+            strengths(2048, 2304, 0)
+            strengths(1024, 1536, 1024)
+            idle()
         for k in (7, 6, 5, 4):
             weigh(k)
         for j in (7, 6, 4):
             base(j)
         for k in (3, 2, 1):
             weigh(k)
-        comp(11)
-        comp(10)
-        comp(9)
+        comp(9, 11)
         votes("K1", 120, 9)
         sgath(7, 7)
         act(row("OWN", 6), r("BX", 0, 320))
@@ -395,104 +407,118 @@ def rank_program(g, core, T, topo):
         tt(r("TT", 120, 240), r("K1", 60, 180), r("C13", 120, 240), A.add)
         tt(r("TT", 60, 120), r("BZ", 0, 60), r("C13", 60, 120), A.add)
         tt(r("M61", 0, 60), r("BZ", 0, 60), r("M60", 0, 60), A.max)
-        ts(sm(NA), r("NU", 0, 20), -10 * U, A.add, U, A.min)
-        ts(r("CN", 60, 240), r("TT", 60, 240), 2047, A.bitwise_and)
+        ts(r("CN", 120, 240), r("TT", 120, 240), 2047, A.bitwise_and)
+        ts(r("CN", 60, 120), r("TT", 60, 120), 2047, A.bitwise_and)
         tt(r("M61", 20, 40), r("M61", 0, 20), r("M61", 20, 40), A.max)
+        cp(r("CH", 120, 240), r("CN", 120, 240))
+        cp(r("CH", 60, 120), r("CN", 60, 120))
+        act(row("OWN", 8), own(8))
+        for k in (7, 5, 3, 1):
+            act(row("OWN", k), own(k + 1))
+        for k in (6, 4, 2):
+            act(wrow(k), r("ZH", 0, 320))
+        if t == 0:
+            act(r("KF", 0, 224), r("KH", 0, 224), F.Identity, 11 * U + C0, -U)
+            act(r("XH", 220, 224), r("K32", 0, 4), F.Identity, 0.0, 0.0)
+            for name, x in (("I16K", 16384), ("N16K", -16384), ("N4K", -4096)):
+                act(r(name, 0, 128), r("ID", 0, 128), F.Identity, 0.0, x)
         mm(r("TOT", 0, 20), r("ID", 0, 128), r("NEG", 0, 20), True, False, False)
-        tt(r("TT", 0, 60), r("BY", 0, 60), r("C13", 0, 60), A.add)
         tt(r("M60", 0, 40), r("BY", 20, 60), r("M61", 20, 60), A.max)
-        cp(r("WB", 60, 240), r("CN", 60, 240))
-        act(row("OWN", 7), r("O8", 0, 320))
-        act(r("B", 16, 336), ind(r("WB", 0, 240), r("LBU", 0, 20)))
-        built = ("a", count["a"])
+        tt(r("TT", 0, 60), r("BY", 0, 60), r("C13", 0, 60), A.add)
+        idle()
         tt(r("KB", 0, 20), r("M60", 0, 20), r("M60", 20, 40), A.max)
         mm(r("TOT", 0, 20), r("GS", 0, 128), r("KB", 0, 20), False, True)
+        field(13, "IH", r("NU", 0, 20))
         tt(sm(KEY), r("M60", 0, 20), r("M60", 20, 40), A.max)
-        ts(r("CN", 0, 60), r("TT", 0, 60), 2047, A.bitwise_and)
+        ts(sm(NA), r("NU", 0, 20), -10 * U, A.add, U, A.min)
+        for k in range(3, 12):
+            field(k, "IH", r("CH", 20 * k, 20 * k + 20))
+        idle()
         ts(sm(THR), r("KB", 0, 20), 824.0, A.is_lt, 1.0e6, A.mult)
+        ts(r("CN", 0, 60), r("TT", 0, 60), 2047, A.bitwise_and)
         cp(r("SI", 0, 20), sm(KEY))
         tt(r("RD", 0, 20), r("TOT", 0, 20), sm(THR), A.is_gt)
-        tt(sm(FR), sm(KEY), r("SI", 0, 20), A.subtract)
-        mm(r("POS", 0, 20), r("TR", 0, 128), r("RD", 0, 20), True, False, False)
+        cp(r("CH", 0, 60), r("CN", 0, 60))
+        tt(r("FR", 0, 20), sm(KEY), r("SI", 0, 20), A.subtract)
+        field(14, "TR", r("RD", 0, 20))
+        for f, x in ((1, r("CH", 20, 40)), (2, r("CH", 40, 60)), (12, r("FR", 0, 20))):
+            field(f, "IH", x)
         emit("v", lambda: g.vector.tensor_tensor_scan(T.CUM[:, 1:21], T.ONE[:, 0:20], T.RD[:, 0:20], 0.0, A.mult, A.add),
              [("ONE", 0, 20), ("RD", 0, 20)], [("CUM", 1, 21)])
-        mm(r("POS", 0, 20), r("NB", 0, 128), r("CUM", 0, 20), False, True)
-        act(r("B", 28, 336, 16), sm(FR), F.Identity, 0.0, 1.0, built)
-        act(row("OWN", 1), row("OWN", 2))
-        cp(r("B", 17, 336, 16), r("CN", 20, 40), built)
-        cp(r("B", 18, 336, 16), r("CN", 40, 60), built)
-        ts(sm(A1), sm(FR), U, A.add, -10240.0, A.mult)
-        tt(sm(DK), sm(FR), sm(NA), A.add)
-        tt(r("B", 29, 336, 16), r("POS", 0, 20), r("NU", 0, 20), A.min, built)
-        ts(sm(SL), r("POS", 0, 20), 0.0, A.is_gt)
-        cp(r("WB", 0, 60), r("CN", 0, 60))
-        tr(r("KW", 0, 320), r("B", 16, 336))
-        tr(r("KW", 320, 672), r("B", 0, 352))
-        act(row("OWN", 3), row("OWN", 4))
-        act(row("OWN", 5), row("OWN", 6))
-        tt(sm(A1), sm(A1), sm(SL), A.mult)
-        tt(sm(DK), sm(DK), sm(SL), A.mult)
+        field(14, "NB", r("CUM", 0, 20), True)
+        ts(sm(A1), r("FR", 0, 20), U, A.add, -10240.0, A.mult)
+        tt(sm(DK), r("FR", 0, 20), sm(NA), A.add)
+        idle()
+        tr(r("KW", 0, 320), r("K2", 16, 336))
+        tr(r("KW", 320, 672), r("K2", 0, 352))
+        ts(sm(SL), r("K2", 30, 336, 16), 0.0, A.is_gt)
         act(r("MK%d" % t, 0, 160), ind(r("KW", 0, 672), r("PL", 0, 10)), F.Relu)
         ts(r("MK%d" % t, 160, 320), ind(r("KW", 0, 672), r("PL", 10, 20)), 0.0, A.max)
         send(t, "MK%d" % t, "RK%d" % t, "rk%d" % t)
         if t == 0:
             load_list()
-        act(row("OWN", 8), r("O8", 0, 320))
+        tt(sm(A1), sm(A1), sm(SL), A.mult)
+        tt(sm(DK), sm(DK), sm(SL), A.mult)
         tt(sm(A2), sm(A1), sm(SC2), A.add)
         tt(sm(NQ0), sm(NA), sm(DK), A.subtract)
-        act(r("DD", 0, 220), r("C", 20, 240), F.Relu, 0.0, -4.0)
+        act(r("DD", 0, 220), r("C", 20, 240), F.Sign, -0.5, -1.0)
         cp(r("AL", 0, 20), sm(A2))
         ts(sm(NQ), sm(NQ0), C0, A.add)
         ts(sm(N4C), sm(NQ0), C0 + 11 * U, A.add)
-        act(r("G1", 0, 220), r("GSC", 0, 220), F.Identity, 997.0 * t - 32768)
-        if t == 0:
-            act(r("KF", 0, 224), r("KV", 0, 224), F.Identity, 11 * U + C0, U)
-            act(r("ZH", 0, 224), r("K32", 0, 224), F.Identity, 0.0, 0.0)
-            act(r("XH", 220, 224), r("K32", 0, 4), F.Identity, 0.0, 0.0)
-            for name, x in (("IF", 1), ("I16K", 16384), ("N16K", -16384), ("N4K", -4096)):
-                act(r(name, 0, 128), r("ID", 0, 128), F.Identity, 0.0, x)
-        mm(r("BY", 0, 220), r("IF", 0, 128), r("WB", 0, 220), True, False, False)
+        act(r("G1", 0, 224), ind(sm(GM), r("LBC", 0, 14)), F.Identity, 997 * t % 2048 - 2048)
+        mm(r("BY", 0, 220), r("IH", 0, 128), r("CH", 0, 220), True, False, False)
         mm(r("BY", 0, 220), r("I16K", 0, 128), r("DD", 0, 220), False, False, False)
-        mm(r("BY", 0, 220), r("IF", 0, 128), r("G1", 0, 220), False, True)
+        mm(r("BY", 0, 220), r("IH", 0, 128), r("G1", 0, 220), False, True)
         room(sm(NQ0))
         under()
         tt(r("LA", 0, 320), ind(r("OWN", 0, 3840), r("AL", 0, 20)), imp, A.subtract)
-        cp(r("CF" if last else "C", 0, 20), r("CN", 0, 20))
+        tt(r("G3", 0, 220), r("BY", 0, 220), r("CH", 20, 240), A.max)
         tt(r("LB", 0, 320), ind(r("WU", 0, 3840), r("AL", 0, 20)), r("LA", 0, 320), A.add)
         act(r("ML%d" % t, 0, 320), ind(r("LB", 0, 320), r("INV", 0, 20)), F.Identity, -OFF)
         send(t, "ML%d" % t, "RL%d" % t, "rl%d" % t)
-        tt(r("G3", 0, 220), r("BY", 0, 220), r("CN", 20, 240), A.max)
+        act(r("CF" if last else "C", 0, 20), r("CH", 0, 20))
         ts(r("G4", 0, 220), r("G3", 0, 220), 2047, A.bitwise_and)
-        mm(r("BX", 0, 220), r("IH", 0, 128), r("ZH", 0, 220), True, False, False)
         arrival(t, "RK%d" % t, "rk%d" % t)
         arrival(t, "RL%d" % t, "rl%d" % t)
         tr(r("XT", 0, 320), r("RK%d" % t, 0, 320))
-        for k in range(1, 12):
-            mm(r("BX", 20 * k - 20, 20 * k), r("IH", 0, 128), r("XT", k, 320, 16), False, k == 11, k == 11)
+        for bank, k0, k1 in (("BX", 1, 7), ("POS", 7, 12)):
+            for k in range(k0, k1):
+                mm(r(bank, 20 * (k - k0), 20 * (k - k0) + 20), r("IH", 0, 128), r("XT", k, 320, 16), k == k0, k == k1 - 1, k == k1 - 1)
+            act(r("XH", 20 * k0 - 20, 20 * k1 - 20), r(bank, 0, 20 * (k1 - k0)), F.Identity, -CA - 0.125, 1.0 / 16384)
         mm(r("K3", 0, 220), r("N4K", 0, 128), r("LM", 0, 220), True, False)
-        act(r("XH", 0, 220), r("BX", 0, 220), F.Identity, -CA - 0.125, 1.0 / 16384)
         tt(sm(D), r("XT", 12, 320, 16), sm(NQ), A.add)
+        tt(sm(E2), r("XT", 13, 320, 16), r("XT", 14, 320, 16), A.min)
         ts(sm(M), sm(D), CA - 2 * U, A.is_lt, 11 * U, A.mult)
-        tt(sm(E2), r("XT", 13, 320, 16), sm(D), A.add)
+        tt(sm(E2), sm(E2), sm(D), A.add)
         tt(r("AH", 0, 20), sm(D), sm(M), A.add)
         tt(sm(BETA), sm(D), sm(M), A.add)
         tt(sm(T1), sm(E2), sm(N4C), A.max)
+        ts(r("AB", 0, 20), r("AH", 0, 20), -CA - 0.125, A.add)
         tt(sm(BQ), sm(BETA), r("AH", 0, 20), A.subtract)
         tt(r("Y1", 0, 224), ind(r("AH", 0, 20), r("LBC", 0, 14)), r("XH", 0, 224), A.add)
-        act(r("AB", 0, 224), ind(r("AH", 0, 20), r("LBC", 0, 14)), F.Identity, 16384 * (CA + 0.125), -16384.0)
         act(r("BB", 0, 224), ind(sm(BQ), r("LBC", 0, 14)), F.Identity, -1024.0, 65536.0)
+        ts(r("NU", 0, 20), sm(T1), -C0, A.add, 12 * U, A.min)
+        if last:
+            ts(sm(TMP), sm(T1), -C0, A.add, 32.0, A.mult)
         for bank, lo, hi in HALVES:
-            mm(r(bank, 0, hi - lo), r("IH", 0, 128), r("AB", lo, hi), True, False, False)
-        ts(r("Z1", 0, 220), r("Y1", 0, 220), 0.0, A.max, 0.125, A.min)
-        ts(r("Z2", 0, 220), r("Y1", 0, 220), -0.125, A.add, 0.0, A.max)
-        act(r("Z0", 0, 220), r("Y1", 0, 220), F.Relu, 0.0, -1.0)
-        cap()
+            for at in range(0, hi - lo, 20):
+                mm(r(bank, at, at + 20), r("N16K", 0, 128), r("AB", 0, 20), at == 0, False, False)
         for bank, lo, hi in HALVES:
             mm(r(bank, 0, hi - lo), r("IH", 0, 128), r("BB", lo, hi), False, False, False)
-        turn(HALVES, "Z1", 0, 220, 7, "I16K")
+        ts(r("Z1", 0, 80), r("Y1", 0, 80), 0.0, A.max, 0.125, A.min)
+        ts(r("Z1", 80, 220), r("Y1", 80, 220), 0.0, A.max, 0.125, A.min)
+        ts(r("Z2", 0, 120), r("Y1", 0, 120), -0.125, A.add, 0.0, A.max)
+        act(r("Z0", 0, 220), r("Y1", 0, 220), F.Relu, 0.0, -1.0)
+        act(r("Z2", 120, 220), r("Y1", 120, 220), F.Relu, -0.125)
+        cap()
+        turn(HALVES, "Z1", 0, 80, 7, "I16K")
+        turn(HALVES, "Z1", 80, 220, 7, "I16K")
         turn(HALVES, "Z0", 0, 220, 3, "N16K")
         turn(HALVES, "Z2", 0, 220, 0, "I16K", True)
         tt(r("UP", 0, 224), ind(sm(E2), r("LBC", 0, 14)), r("KF", 0, 224), A.is_le)
+        if last:
+            ts(sm(T2), sm(TMP), 12.0, A.min)
+            store("s", "d_yn", T.yn[:], sm(T2))
         mm(r("K3", 0, 220), r("NH", 0, 128), r("BB", 0, 220), False, False)
         mm(r("K3", 0, 220), r("N4K", 0, 128), r("UP", 0, 220), False, False)
         for h in (0, 1):
@@ -507,15 +533,12 @@ def rank_program(g, core, T, topo):
             turn(WHOLE, "Z4", lo, hi, 10, "IH")
             turn(WHOLE, "Z6", lo2, hi2, 0, "IH", h == 1)
         tt(r("BASE", 0, 220), r("G4", 0, 220), r("K1", 0, 220), A.min)
-        ts(r("NU", 0, 20), sm(T1), -C0, A.add, 12 * U, A.min)
         if not last:
             act(row("OWN", 12), r("RL%d" % t, 0, 320))
         else:
             act(r("YI", 0, 320), r("RL%d" % t, 0, 320), F.Identity, OFF)
             store("a", "d_yi", T.yi[:], r("YI", 0, 320))
-            ts(sm(TMP), r("NU", 0, 20), 32.0, A.mult)
-            store("s", "d_yn", T.yn[:], sm(TMP))
-        for lo, hi in (((0, 220),) if last else ((140, 220), (0, 140))):
+        for lo, hi in (((0, 220),) if last else ((120, 220), (0, 120))):
             tt(r("CF" if last else "C", 20 + lo, 20 + hi), r("K3", lo, hi), r("BASE", lo, hi), A.max)
 
     store("s", "d_yc", T.yc[:], r("CF", 0, 240))

from concourse.mybir import AluOpType, ActivationFunctionType

A = AluOpType
F = ActivationFunctionType
RO = 4
OFF = 1792.0
BIG = 65536.0
U = 1.0 / 32
CA = 24.0
C0 = CA - 1.5 * U

SCRATCH = {}
for _dt, _bufs in (
        ("int32", dict(CS=240, NS=32, DS=32, P=224, Q=224, TT=240, CN=240, SI=32, SJ=64, G3=240, G4=240, PC=8, HJ=16)),
        ("bfloat16", dict(WT=2064, ST=2048, S16=2320, WU=3840, SG=2240, OVER=3840, KB=32, RD=32, CUM=32,
                          Z=144, ID=128, NI=128, GS=128, BO=128, TR=128, NB=128, KK=240, NEG=32, ONE=128, X=128, AH=32, KH=224)),
        ("float16", dict(C=256, IMP=320, XT=320, O8=320, IH=128, NH=128, I16K=128, N16K=128, N4K=128, K32=224, ZH=352,
                         N4=224, DD=224, AB=224, BB=224, UP=224, LM=224, Z0=224, Z1=224, Z2=224, Z3=224, Z4=224,
                         Z5=224, Z6=224, NU=32, FR=32, CH=240, G1=224)),
        ("uint16", dict(WI=224, HI=224, AL=32, INV=32, PL=32, LBC=16)),
        ("float32", dict(CF=256, OWN=3840, LA=320, LB=320, C13=240, KS=128, M60=64, M61=64, SM=768,
                         KW=672, Y=352, BASE=224, YI=320, PF=16, KF=224,
                         XH=224, Y1=224, J4=32, H=64))):
    for _n, _w in _bufs.items():
        SCRATCH[_n] = ("sbuf", [128, _w], _dt)
PSUM = ("POS", "BX", "BY", "BZ", "K1", "K2", "K3", "TOT")
for _n in PSUM:
    SCRATCH[_n] = ("psum", [128, 512], "float32")
for _t in range(RO):
    for _n in ("MK", "RK", "ML", "RL"):
        SCRATCH["%s%d" % (_n, _t)] = ("sbuf", [128, 320], "float16")
SEMAPHORES = (["v", "a", "t", "p", "sent", "d_cs", "d_ns", "d_ds", "d_wt", "d_s0", "d_s1", "d_yc", "d_yn", "d_yi"]
              + ["rk%d" % t for t in range(RO)] + ["rl%d" % t for t in range(RO)])


def rank_program(g, core, T, topo):
    rank = T.rank_of(core)
    if rank is None:
        return
    n_ranks = len(T.cores)
    eng = {"v": g.vector, "a": g.scalar, "t": g.tensor, "p": g, "s": g.sync}
    count = {"v": 0, "a": 0, "t": 0, "p": 0}
    known = {q: {} for q in eng}
    snap = {}
    log = {}

    def r(name, lo, hi, step=1):
        ap = T[name][:, lo:hi] if step == 1 else T[name][:, lo:hi:step]
        if name in PSUM:
            return ap, [(name, 0, 512)]
        return ap, [(name, lo, hi)]

    def ind(win, off):
        return win[0].indirect(off[0]), win[1] + off[1]

    def sm(i):
        return r("SM", 32 * i, 32 * i + 20)

    def wait(q, sem, val):
        if known[q].get(sem, 0) >= val:
            return
        eng[q].wait_ge(T.sem[sem], val)
        known[q][sem] = val
        for s2, v2 in snap.get((sem, val), {}).items():
            if known[q].get(s2, 0) < v2:
                known[q][s2] = v2

    def order(q, reads, writes):
        need = {}
        for rs, w in ((reads, False), (writes, True)):
            for name, lo, hi in rs:
                ps = name in PSUM
                for lo2, hi2, w2, sem, val in log.get(name, []):
                    if lo < hi2 and lo2 < hi and (w or w2 or (ps and sem != q)):
                        if q == "t" and sem == "t":
                            continue
                        need[sem] = max(need.get(sem, 0), val)
        for sem in sorted(need, key=lambda s: s == q):
            wait(q, sem, need[sem])

    def note(q, reads, writes, sem, val, keep=False):
        snap[(sem, val)] = dict(known[q])
        for name, lo, hi in writes:
            log[name] = [e for e in log.get(name, []) if keep or not (lo <= e[0] and e[1] <= hi)] + [(lo, hi, True, sem, val)]
        for name, lo, hi in reads:
            log[name] = [e for e in log.get(name, []) if not (e[3] == sem and not e[2] and lo <= e[0] and e[1] <= hi)]
            log[name].append((lo, hi, False, sem, val))

    def emit(q, make, reads, writes, inc=True, apart=None):
        if apart is None:
            order(q, reads, writes)
        else:
            order(q, reads, [])
            wait(q, apart[0], apart[1])
        ins = make()
        if inc:
            count[q] += 1
            ins.then_inc(T.sem[q], 1)
            note(q, reads, writes, q, count[q], apart is not None)
        else:
            note(q, reads, writes, q, count[q] + 1)

    def tt(out, a, b, op, apart=None):
        emit("v", lambda: g.vector.tensor_tensor(out[0], a[0], b[0], op), a[1] + b[1], out[1], True, apart)

    def ts(out, a, s1, op0, s2=None, op1=None, apart=None):
        rd = a[1] + (s1[1] if isinstance(s1, tuple) else []) + (s2[1] if isinstance(s2, tuple) else [])
        x1 = s1[0] if isinstance(s1, tuple) else s1
        x2 = s2[0] if isinstance(s2, tuple) else s2
        if op1 is None:
            emit("v", lambda: g.vector.tensor_scalar(out[0], a[0], x1, None, op0), rd, out[1], True, apart)
        else:
            emit("v", lambda: g.vector.tensor_scalar(out[0], a[0], x1, x2, op0, op1), rd, out[1], True, apart)

    def cp(out, a, apart=None):
        emit("v", lambda: g.vector.tensor_copy(out[0], a[0]), a[1], out[1], True, apart)

    def tr(out, a):
        emit("v", lambda: g.vector.transpose(out[0], a[0]), a[1], out[1])

    def fill(out, val):
        emit("v", lambda: g.vector.memset(out[0], val), [], out[1])

    def act(out, a, func=F.Identity, bias=0.0, scale=1.0, apart=None):
        emit("a", lambda: g.scalar.activation(out[0], a[0], func, bias=float(bias), scale=float(scale)), a[1], out[1], True, apart)

    def mm(out, lhs, rhs, start, stop, inc=True):
        emit("t", lambda: g.tensor.matmul(out[0], lhs[0], rhs[0], start, stop), lhs[1] + rhs[1], out[1], inc)

    def iota(out, pattern, base, mult=0, flt=True):
        if flt:
            emit("p", lambda: g.iota(out[0], pattern, base, mult, allow_small_or_imprecise_dtypes=True), [], out[1])
        else:
            emit("p", lambda: g.iota(out[0], pattern, base, mult), [], out[1])

    def pick(out, a, pattern, op, base, mult, other=0.0):
        emit("p", lambda: g.affine_select(out[0], a[0], pattern, op, other, base, mult), a[1], out[1])

    def load(q, sem, dst, src):
        eng[q].dma_start(dst[0], src).then_inc(T.sem[sem], 16)
        note(q, [], dst[1], sem, 16)

    def store(q, sem, dst, src):
        order(q, src[1], [])
        eng[q].dma_start(dst, src[0]).then_inc(T.sem[sem], 16)

    sent = [0]

    def send(t, src, dst, sem):
        to = T.cores[(rank + 1 + t % (n_ranks - 1)) % n_ranks]
        rid, pid = topo.addr(to, core)
        order("p", [(src, 0, 320)], [])
        g.remote_dma(T[dst][:], T[src][:], T.sem[sem], T.sem.sent, pid, rid, topo.mask(core, to))
        sent[0] += len(topo.engines(core, to))

    def arrival(t, name, sem):
        frm = T.cores[(rank - 1 - t % (n_ranks - 1)) % n_ranks]
        log[name] = [(0, 320, True, sem, len(topo.engines(frm, core)))]

    (KEY, THR, FR, SL, A1, A2, NA, DK, NQ0, NQ, N4C, D, M, BETA, BQ, E2, SC, SC2, TMP, PM, T1, T2, GM) = range(23)

    load("s", "d_ns", r("NS", 0, 20), T.ns[:])
    load("a", "d_ds", r("DS", 0, 20), T.ds[:])
    load("s", "d_cs", r("CS", 0, 240), T.cs[:])
    load("s", "d_wt", r("WT", 16, 2064), T.wt[:])
    load("s", "d_s0", r("ST", 0, 1024), T.st[:, 0:1024])
    load("s", "d_s1", r("ST", 1024, 2048), T.st[:, 1024:2048])

    iota(r("PC", 0, 1), [[0, 1]], 0, 1, False)
    iota(r("H", 0, 16), [[16, 16]], 0)
    fill(r("ONE", 0, 128), 1.0)
    fill(r("IMP", 0, 320), -OFF)
    fill(r("WT", 0, 16), 0.0)
    pick(r("ID", 0, 128), r("ONE", 0, 128), [[-1, 128]], A.is_equal, 0, 1)
    iota(r("YI", 0, 320), [[32, 10], [1024, 2], [1, 16]], 0)
    iota(r("KH", 0, 220), [[-1, 11], [0, 20]], 10)
    iota(r("J4", 0, 20), [[1, 20]], 0)
    act(r("K32", 0, 224), r("IMP", 0, 224), F.Identity, 32.0, 0.0)
    act(r("ZH", 0, 176), r("IMP", 0, 176), F.Identity, 0.0, 0.0)
    act(r("ZH", 176, 352), r("IMP", 0, 176), F.Identity, 0.0, 0.0)
    act(r("IH", 0, 128), r("ID", 0, 128))
    act(r("NI", 0, 128), r("ID", 0, 128), F.Identity, 0.0, -1.0)
    act(r("Z", 0, 144), r("IMP", 0, 144), F.Identity, 0.0, 0.0)
    act(r("OVER", 0, 320), r("IMP", 0, 320), F.Identity, 0.0, 0.0)
    act(r("Y", 0, 16), r("IMP", 0, 16), F.Identity, 0.0, 0.0)
    act(r("Y", 336, 352), r("IMP", 0, 16), F.Identity, 0.0, 0.0)
    act(r("KH", 220, 224), r("IMP", 0, 4), F.Identity, 0.0, 0.0)
    act(r("NEG", 0, 32), r("IMP", 0, 32), F.Identity, -7328.0, 0.0)
    act(r("CUM", 0, 32), r("IMP", 0, 32), F.Identity, 0.0, 0.0)
    act(r("NH", 0, 128), r("ID", 0, 128), F.Identity, 0.0, -1.0)
    act(r("OWN", 3520, 3840), r("IMP", 0, 320))
    pick(r("X", 0, 128), r("ONE", 0, 128), [[0, 8], [-1, 16]], A.is_equal, 0, 1)
    pick(r("BO", 0, 128), r("ONE", 0, 128), [[-16, 8], [0, 16]], A.is_ge, 0, 1)
    pick(r("BO", 0, 128), r("BO", 0, 128), [[16, 8], [0, 16]], A.is_ge, 15, -1)
    iota(r("KK", 0, 240), [[-1, 12], [0, 20]], 11)
    iota(sm(PM), [[0, 10], [16, 2]], 0)

    def room(height):
        act(r("N4", 0, 224), ind(height, r("LBC", 0, 14)), F.Identity, 0.0, 32.0)
        mm(r("K2", 0, 220), r("ID", 0, 128), r("KH", 0, 220), True, False, False)
        mm(r("K2", 0, 220), r("IH", 0, 128), r("N4", 0, 220), False, True)

    def under():
        act(r("LM", 0, 220), r("K2", 0, 220), F.Relu)

    def cap():
        act(r("K1", 0, 220), r("LM", 0, 220), F.Identity, -1.0, 4096.0)

    ts(r("PC", 1, 2), r("PC", 0, 1), 15, A.bitwise_and)
    ts(r("PC", 2, 3), r("PC", 0, 1), 16, A.bitwise_and)
    fill(r("S16", 2304, 2320), 1.0e6)
    cp(r("PF", 0, 3), r("PC", 0, 3))
    rc = r("PF", 1, 2)
    ts(r("H", 0, 16), r("H", 0, 16), rc, A.add)
    ts(r("PF", 6, 7), r("PF", 2, 3), 64.0, A.mult)
    ts(r("PF", 7, 8), r("PF", 2, 3), -2.0, A.mult, 352.0, A.add)
    ts(r("HJ", 0, 16), r("H", 0, 16), -9.5, A.add, 0.05, A.mult)
    cp(r("AL", 0, 20), r("DS", 0, 20))
    ts(r("KB", 0, 20), r("NS", 0, 20), -11.5, A.add)
    ts(r("NU", 0, 20), r("NS", 0, 20), U, A.mult)
    emit("v", lambda: g.vector.tensor_copy(ind(r("Y", 16, 336), r("AL", 0, 20))[0], T.YI[:, 0:320]),
         [("YI", 0, 320), ("AL", 0, 20)], [("Y", 16, 336)])
    mm(r("K2", 0, 352), r("IH", 0, 128), r("ZH", 0, 352), True, True)
    for at in range(0, 220, 20):
        mm(r("K1", at, at + 20), r("ID", 0, 128), r("KB", 0, 20), at == 0, False, False)
    mm(r("K1", 0, 220), r("ID", 0, 128), r("KH", 0, 220), False, True)
    ts(r("K3", 0, 220), r("K1", 0, 220), -1.0 / 4096, A.max, 4096.0, A.mult)
    cp(r("C", 0, 20), r("CS", 0, 20))
    ts(sm(SC), r("J4", 0, 20), 16.0, A.mult, rc, A.add)
    tt(r("C", 20, 240), r("K3", 0, 220), r("CS", 20, 240), A.min)

    def matrices():
        mm(r("TOT", 0, 128), r("X", 0, 128), r("X", 0, 128), True, True)
        act(r("GS", 0, 128), r("TOT", 0, 128))
        act(r("Z", 15, 143, 16), r("BO", 0, 128, 16), F.Identity, 0.0, 97.0)
        act(r("NB", 0, 128), r("BO", 0, 128), F.Identity, 0.0, -1.0)
        pick(r("TR", 0, 128), r("NB", 0, 128), [[1, 128]], A.is_gt, 0, -1)
        pick(r("TR", 0, 128), r("TR", 0, 128), [[1, 128]], A.not_equal, 0, -1, 80.0)
        iota(r("WU", 7 * 320, 12 * 320), [[0, 5 * 320]], 0)

    spare = [lambda: tr(r("KW", 0, 320), r("Y", 16, 336)),
             lambda: cp(r("SJ", 0, 20), r("KW", 0, 320, 16)),
             lambda: cp(sm(T2), r("KW", 0, 320, 16)),
             lambda: ts(r("SJ", 20, 40), r("SJ", 0, 20), 1024, A.bitwise_and),
             lambda: ts(r("SJ", 40, 60), r("SJ", 0, 20), 1023, A.bitwise_and),
             lambda: ts(sm(T1), r("SJ", 20, 40), r("PF", 6, 7), A.not_equal, r("PF", 7, 8), A.mult),
             lambda: ts(r("SJ", 41, 60, 2), r("SJ", 41, 60, 2), 16.0, A.add),
             lambda: tt(sm(T1), sm(T1), r("SJ", 40, 60), A.add),
             lambda: cp(r("PL", 0, 20), sm(T1))]

    def idle(n=1):
        for _ in range(min(n, len(spare))):
            spare.pop(0)()

    def load_list():
        tr(r("KW", 320, 672), r("Y", 0, 352))
        ts(sm(PM), sm(PM), r("PF", 2, 3), A.not_equal)
        ts(r("H", 16, 32), r("HJ", 0, 16), -20.0, A.mult)
        tt(sm(T1), r("KW", 336, 656, 16), sm(T2), A.subtract)
        ts(r("SJ", 0, 20), sm(SC), 31.0, A.mult)
        tt(r("H", 32, 48), r("H", 16, 32), r("H", 0, 16), A.add)
        tt(sm(T1), sm(T1), sm(PM), A.mult)
        ts(r("SJ", 20, 40), r("SJ", 0, 20), 2047, A.bitwise_and)
        cp(r("LBC", 0, 16), r("H", 32, 48))
        tt(sm(T1), sm(T1), sm(T2), A.add)
        cp(sm(GM), r("SJ", 20, 40))
        ts(sm(SC2), sm(SC), 3520.0, A.add)
        ts(sm(T2), sm(T1), 1023.5, A.is_gt, -1008.0, A.mult)
        tt(sm(T1), sm(T1), sm(T2), A.add)
        cp(r("INV", 0, 20), sm(T1))

    def row(name, k):
        return r(name, (k - 1) * 320, k * 320)

    def wrow(k):
        return row("WU", k)

    def wgath(lo, hi):
        act(r("WU", (lo - 1) * 320, hi * 320), ind(r("WT", 0, 2064), r("WI", 20 * (lo - 1), 20 * hi)))

    def sgath(lo, hi):
        act(r("SG", (lo - 1) * 320, hi * 320), ind(r("S16", 0, 2320), r("HI", 20 * (lo - 1), 20 * hi)))

    SUMS = {7: "BY", 6: "BX", 4: "BZ"}
    GAPS = {5: "TOT", 3: "POS", 1: "K3"}

    def weigh(k):
        for j in sorted(SUMS, reverse=True):
            if j <= k:
                mm(r(SUMS[j], 0, 320), r("ID", 0, 128), wrow(k), k == 7, False, False)
        if k in (3, 2):
            mm(r("K2", 0, 320), r("ID", 0, 128), wrow(k), k == 3, k == 2, k == 2)
        if k in GAPS:
            mm(r(GAPS[k], 0, 320), r("NI", 0, 128), wrow(k), True, False, False)

    def base(j):
        mm(r(SUMS[j], 0, 320), r("IH", 0, 128), r("O8", 0, 320), False, True)

    def gap(k):
        mm(r(GAPS[k], 0, 320), r("ID", 0, 128), row("SG", k), False, True)

    def own(k):
        return r("O8", 0, 320) if k == 8 else row("OWN", k)

    def chain(k, imp=None):
        tt(own(k), ind(r("WT", 0, 2064), r("WI", 20 * (k - 1), 20 * k)), imp or own(k + 1), A.add)

    def over(k):
        if k in GAPS:
            tt(r("OVER", k * 320, k * 320 + 320), r(GAPS[k], 0, 320), own(k + 1), A.is_lt)
        else:
            tt(r("OVER", k * 320, k * 320 + 320), row("SG", k), r(SUMS[k], 0, 320), A.is_lt)

    def comp(k, hi=None):
        loads = r("OWN", (k - 1) * 320, hi * 320) if hi else own(k)
        hi = hi or k
        tt(r("OVER", k * 320, hi * 320 + 320), ind(r("S16", 0, 2320), r("HI", 20 * (k - 1), 20 * hi)), loads, A.is_lt)

    def votes(bank, at, k0):
        kp = r(bank, at, at + 60)
        mm(kp, r("ID", 0, 128), r("KK", 20 * k0, 20 * k0 + 60), True, False, False)
        for j in range(16):
            mm(kp, r("Z", 15 - j, 143 - j), r("OVER", k0 * 320 + j, (k0 + 3) * 320, 16), False, j == 15, j == 15)

    def strengths(lo, hi, frm):
        ts(r("S16", lo, hi), r("ST", frm, frm + hi - lo), 16.0, A.mult, -OFF, A.add)

    def field(f, lhs, x, stop=False):
        mm(r("K2", 16 + f, 336, 16), r(lhs, 0, 128), x, f == 13, stop, stop)

    HALVES = (("BZ", 0, 120), ("TOT", 120, 220))
    WHOLE = (("K3", 0, 220),)

    def turn(banks, z, lo, hi, s, lhs, stop=False):
        for bank, b0, b1 in banks:
            cuts = [(max(lo + w, b0), min(hi + w, b1), w) for w in (20 * s, 20 * s - 220)]
            cuts = [c for c in cuts if c[0] < c[1]]
            for i, (a, b, w) in enumerate(cuts):
                end = stop and i == len(cuts) - 1
                mm(r(bank, a - b0, b - b0), r(lhs, 0, 128), r(z, a - w, b - w), False, end, end)

    for t in range(RO):
        last = t == RO - 1
        imp = r("IMP", 0, 320) if t == 0 else r("RL%d" % (t - 1), 0, 320)
        ts(r("WI", 120, 220), r("C", 140, 240), 16.0, A.add)
        ts(r("WI", 0, 120), r("C", 20, 140), 16.0, A.add)
        mm(r("POS", 0, 220), r("IH", 0, 128), r("K32", 0, 220), True, False, False)
        mm(r("POS", 0, 220), r("IH", 0, 128), r("C", 0, 220), False, True)
        for lo, hi in ((7, 7), (5, 6), (3, 4), (1, 2)):
            if t == 0 and lo == 7:
                matrices()
            if t == 0 and lo == 5:
                act(r("KK", 0, 240), r("KK", 0, 240), F.Identity, 0.0, U)
            if t == 0 and lo == 1:
                act(r("S16", 1536, 2048), r("ST", 1536, 2048), F.Identity, -OFF, 16.0)
            wgath(lo, hi)
        lists = (lambda: tt(r("P", 0, 220), r("C", 20, 240), r("POS", 0, 220), A.mult),
                 lambda: ts(r("Q", 0, 220), r("P", 0, 220), 5, A.arith_shift_right, 2047 | (1 << 20), A.bitwise_and),
                 lambda: ts(r("HI", 0, 220), r("Q", 0, 220), 77.0 * t, A.add, 2304.0, A.min))
        if t == 0:
            for make in lists[:2]:
                idle()
                make()
            lists = (lists[2], lambda: idle(3), lambda: strengths(0, 1024, 0))
        chain(11, imp)
        for k in (10, 9, 8):
            lists[10 - k]()
            chain(k)
        if t == 0:
            strengths(2048, 2304, 0)
            strengths(1024, 1536, 1024)
            idle()
        for k in (7, 6, 5, 4):
            weigh(k)
        for j in (7, 6, 4):
            base(j)
        for k in (3, 2, 1):
            weigh(k)
        comp(9, 11)
        votes("K1", 120, 9)
        sgath(7, 7)
        act(row("OWN", 6), r("BX", 0, 320))
        sgath(5, 5)
        gap(5)
        act(row("OWN", 4), r("BZ", 0, 320))
        sgath(3, 3)
        sgath(2, 2)
        sgath(1, 1)
        comp(8)
        over(7)
        comp(6)
        votes("K1", 60, 6)
        gap(3)
        over(5)
        comp(4)
        mm(r("BX", 0, 320), r("ID", 0, 128), row("SG", 2), True, True)
        tt(row("OWN", 2), r("K2", 0, 320), row("OWN", 4), A.add)
        over(3)
        gap(1)
        votes("BZ", 0, 3)
        act(r("KS", 60, 120), r("K1", 120, 180))
        act(r("C13", 0, 240), r("C", 0, 240), F.Identity, float(t), 13.0)
        tt(r("OVER", 640, 960), r("BX", 0, 320), row("OWN", 2), A.is_lt)
        over(1)
        votes("BY", 0, 0)
        tt(r("M60", 0, 60), r("K1", 60, 120), r("KS", 60, 120), A.max)
        tt(r("TT", 120, 240), r("K1", 60, 180), r("C13", 120, 240), A.add)
        tt(r("TT", 60, 120), r("BZ", 0, 60), r("C13", 60, 120), A.add)
        tt(r("M61", 0, 60), r("BZ", 0, 60), r("M60", 0, 60), A.max)
        ts(r("CN", 120, 240), r("TT", 120, 240), 2047, A.bitwise_and)
        ts(r("CN", 60, 120), r("TT", 60, 120), 2047, A.bitwise_and)
        tt(r("M61", 20, 40), r("M61", 0, 20), r("M61", 20, 40), A.max)
        cp(r("CH", 120, 240), r("CN", 120, 240))
        cp(r("CH", 60, 120), r("CN", 60, 120))
        act(row("OWN", 8), own(8))
        for k in (7, 5, 3, 1):
            act(row("OWN", k), own(k + 1))
        for k in (6, 4, 2):
            act(wrow(k), r("ZH", 0, 320))
        if t == 0:
            act(r("KF", 0, 224), r("KH", 0, 224), F.Identity, 11 * U + C0, -U)
            act(r("XH", 220, 224), r("K32", 0, 4), F.Identity, 0.0, 0.0)
            for name, x in (("I16K", 16384), ("N16K", -16384), ("N4K", -4096)):
                act(r(name, 0, 128), r("ID", 0, 128), F.Identity, 0.0, x)
        mm(r("TOT", 0, 20), r("ID", 0, 128), r("NEG", 0, 20), True, False, False)
        tt(r("M60", 0, 40), r("BY", 20, 60), r("M61", 20, 60), A.max)
        tt(r("TT", 0, 60), r("BY", 0, 60), r("C13", 0, 60), A.add)
        idle()
        tt(r("KB", 0, 20), r("M60", 0, 20), r("M60", 20, 40), A.max)
        mm(r("TOT", 0, 20), r("GS", 0, 128), r("KB", 0, 20), False, True)
        field(13, "IH", r("NU", 0, 20))
        tt(sm(KEY), r("M60", 0, 20), r("M60", 20, 40), A.max)
        ts(sm(NA), r("NU", 0, 20), -10 * U, A.add, U, A.min)
        for k in range(3, 12):
            field(k, "IH", r("CH", 20 * k, 20 * k + 20))
        idle()
        ts(sm(THR), r("KB", 0, 20), 824.0, A.is_lt, 1.0e6, A.mult)
        ts(r("CN", 0, 60), r("TT", 0, 60), 2047, A.bitwise_and)
        cp(r("SI", 0, 20), sm(KEY))
        tt(r("RD", 0, 20), r("TOT", 0, 20), sm(THR), A.is_gt)
        cp(r("CH", 0, 60), r("CN", 0, 60))
        tt(r("FR", 0, 20), sm(KEY), r("SI", 0, 20), A.subtract)
        field(14, "TR", r("RD", 0, 20))
        for f, x in ((1, r("CH", 20, 40)), (2, r("CH", 40, 60)), (12, r("FR", 0, 20))):
            field(f, "IH", x)
        emit("v", lambda: g.vector.tensor_tensor_scan(T.CUM[:, 1:21], T.ONE[:, 0:20], T.RD[:, 0:20], 0.0, A.mult, A.add),
             [("ONE", 0, 20), ("RD", 0, 20)], [("CUM", 1, 21)])
        field(14, "NB", r("CUM", 0, 20), True)
        ts(sm(A1), r("FR", 0, 20), U, A.add, -10240.0, A.mult)
        tt(sm(DK), r("FR", 0, 20), sm(NA), A.add)
        idle()
        tr(r("KW", 0, 320), r("K2", 16, 336))
        tr(r("KW", 320, 672), r("K2", 0, 352))
        ts(sm(SL), r("K2", 30, 336, 16), 0.0, A.is_gt)
        act(r("MK%d" % t, 0, 160), ind(r("KW", 0, 672), r("PL", 0, 10)), F.Relu)
        ts(r("MK%d" % t, 160, 320), ind(r("KW", 0, 672), r("PL", 10, 20)), 0.0, A.max)
        send(t, "MK%d" % t, "RK%d" % t, "rk%d" % t)
        if t == 0:
            load_list()
        tt(sm(A1), sm(A1), sm(SL), A.mult)
        tt(sm(DK), sm(DK), sm(SL), A.mult)
        tt(sm(A2), sm(A1), sm(SC2), A.add)
        tt(sm(NQ0), sm(NA), sm(DK), A.subtract)
        act(r("DD", 0, 220), r("C", 20, 240), F.Sign, -0.5, -1.0)
        cp(r("AL", 0, 20), sm(A2))
        ts(sm(NQ), sm(NQ0), C0, A.add)
        ts(sm(N4C), sm(NQ0), C0 + 11 * U, A.add)
        act(r("G1", 0, 224), ind(sm(GM), r("LBC", 0, 14)), F.Identity, 997 * t % 2048 - 2048)
        mm(r("BY", 0, 220), r("IH", 0, 128), r("CH", 0, 220), True, False, False)
        mm(r("BY", 0, 220), r("I16K", 0, 128), r("DD", 0, 220), False, False, False)
        mm(r("BY", 0, 220), r("IH", 0, 128), r("G1", 0, 220), False, True)
        room(sm(NQ0))
        under()
        tt(r("LA", 0, 320), ind(r("OWN", 0, 3840), r("AL", 0, 20)), imp, A.subtract)
        tt(r("G3", 0, 220), r("BY", 0, 220), r("CH", 20, 240), A.max)
        tt(r("LB", 0, 320), ind(r("WU", 0, 3840), r("AL", 0, 20)), r("LA", 0, 320), A.add)
        act(r("ML%d" % t, 0, 320), ind(r("LB", 0, 320), r("INV", 0, 20)), F.Identity, -OFF)
        send(t, "ML%d" % t, "RL%d" % t, "rl%d" % t)
        act(r("CF" if last else "C", 0, 20), r("CH", 0, 20))
        ts(r("G4", 0, 220), r("G3", 0, 220), 2047, A.bitwise_and)
        arrival(t, "RK%d" % t, "rk%d" % t)
        arrival(t, "RL%d" % t, "rl%d" % t)
        tr(r("XT", 0, 320), r("RK%d" % t, 0, 320))
        for bank, k0, k1 in (("BX", 1, 7), ("POS", 7, 12)):
            for k in range(k0, k1):
                mm(r(bank, 20 * (k - k0), 20 * (k - k0) + 20), r("IH", 0, 128), r("XT", k, 320, 16), k == k0, k == k1 - 1, k == k1 - 1)
            act(r("XH", 20 * k0 - 20, 20 * k1 - 20), r(bank, 0, 20 * (k1 - k0)), F.Identity, -CA - 0.125, 1.0 / 16384)
        mm(r("K3", 0, 220), r("N4K", 0, 128), r("LM", 0, 220), True, False)
        tt(sm(D), r("XT", 12, 320, 16), sm(NQ), A.add)
        tt(sm(E2), r("XT", 13, 320, 16), r("XT", 14, 320, 16), A.min)
        ts(sm(M), sm(D), CA - 2 * U, A.is_lt, 11 * U, A.mult)
        tt(sm(E2), sm(E2), sm(D), A.add)
        tt(r("AH", 0, 20), sm(D), sm(M), A.add)
        tt(sm(BETA), sm(D), sm(M), A.add)
        tt(sm(T1), sm(E2), sm(N4C), A.max)
        ts(r("AB", 0, 20), r("AH", 0, 20), -CA - 0.125, A.add)
        tt(sm(BQ), sm(BETA), r("AH", 0, 20), A.subtract)
        tt(r("Y1", 0, 224), ind(r("AH", 0, 20), r("LBC", 0, 14)), r("XH", 0, 224), A.add)
        act(r("BB", 0, 224), ind(sm(BQ), r("LBC", 0, 14)), F.Identity, -1024.0, 65536.0)
        ts(r("NU", 0, 20), sm(T1), -C0, A.add, 12 * U, A.min)
        if last:
            ts(sm(TMP), sm(T1), -C0, A.add, 32.0, A.mult)
        for bank, lo, hi in HALVES:
            for at in range(0, hi - lo, 20):
                mm(r(bank, at, at + 20), r("N16K", 0, 128), r("AB", 0, 20), at == 0, False, False)
        for bank, lo, hi in HALVES:
            mm(r(bank, 0, hi - lo), r("IH", 0, 128), r("BB", lo, hi), False, False, False)
        ts(r("Z1", 0, 80), r("Y1", 0, 80), 0.0, A.max, 0.125, A.min)
        ts(r("Z1", 80, 220), r("Y1", 80, 220), 0.0, A.max, 0.125, A.min)
        ts(r("Z2", 0, 120), r("Y1", 0, 120), -0.125, A.add, 0.0, A.max)
        act(r("Z0", 0, 220), r("Y1", 0, 220), F.Relu, 0.0, -1.0)
        act(r("Z2", 120, 220), r("Y1", 120, 220), F.Relu, -0.125)
        cap()
        turn(HALVES, "Z1", 0, 80, 7, "I16K")
        turn(HALVES, "Z1", 80, 220, 7, "I16K")
        turn(HALVES, "Z0", 0, 220, 3, "N16K")
        turn(HALVES, "Z2", 0, 220, 0, "I16K", True)
        tt(r("UP", 0, 224), ind(sm(E2), r("LBC", 0, 14)), r("KF", 0, 224), A.is_le)
        if last:
            ts(sm(T2), sm(TMP), 12.0, A.min)
            store("s", "d_yn", T.yn[:], sm(T2))
        mm(r("K3", 0, 220), r("NH", 0, 128), r("BB", 0, 220), False, False)
        mm(r("K3", 0, 220), r("N4K", 0, 128), r("UP", 0, 220), False, False)
        for h in (0, 1):
            bank, lo, hi = HALVES[h]
            ts(r("Z3", lo, hi), r(bank, 0, hi - lo), -2048.0, A.max, 0.0, A.min)
            ts(r("Z4", lo, hi), r(bank, 0, hi - lo), 0.0, A.max, 2048.0, A.min)
            bank, lo2, hi2 = HALVES[1 - h]
            act(r("Z5", lo2, hi2), r(bank, 0, hi2 - lo2), F.Relu, -2048.0, -1.0)
            act(r("Z6", lo2, hi2), r(bank, 0, hi2 - lo2), F.Relu, -2048.0, 1.0)
            turn(WHOLE, "Z3", lo, hi, 9, "IH")
            turn(WHOLE, "Z5", lo2, hi2, 8, "NH")
            turn(WHOLE, "Z4", lo, hi, 10, "IH")
            turn(WHOLE, "Z6", lo2, hi2, 0, "IH", h == 1)
        tt(r("BASE", 0, 220), r("G4", 0, 220), r("K1", 0, 220), A.min)
        if not last:
            act(row("OWN", 12), r("RL%d" % t, 0, 320))
        else:
            act(r("YI", 0, 320), r("RL%d" % t, 0, 320), F.Identity, OFF)
            store("a", "d_yi", T.yi[:], r("YI", 0, 320))
        for lo, hi in (((0, 220),) if last else ((120, 220), (0, 120))):
            tt(r("CF" if last else "C", 20 + lo, 20 + hi), r("K3", lo, hi), r("BASE", lo, hi), A.max)

    store("s", "d_yc", T.yc[:], r("CF", 0, 240))
    for sem in ("d_yi", "d_yn", "d_yc"):
        wait("s", sem, 16)
    for q in ("v", "a", "t", "p"):
        wait("s", q, count[q])
    g.wait_ge(T.sem.sent, sent[0])
